import numpy as np, ml_dtypes
CORES = [24,48,72,152,176,200]
N = 6
BF = ml_dtypes.bfloat16
def gentries(a):
    return np.ascontiguousarray(a.reshape(8, 16, -1).transpose(0, 2, 1)).reshape(8, -1)
def gtable(e):
    e = np.asarray(e); return np.ascontiguousarray(e.reshape(8, -1, 16).transpose(0, 2, 1)).reshape(128, -1).astype(np.int32)
L, S, T, H, C, X, LG = 1152, 256, 3, 5, 32, 80, 11
W = 2 ** LG; EMPTY = 16 * W - 1; OLD = 8
def parts(rng):
    z = rng.random((N, 8, 3, L)); p = 1.3 * rng.random((N, 8, 3, T * S)) - 0.15; mix = 220 * (2 * rng.random((N, 8, 16, 3)) - 1)
    w = np.clip(np.rint(128 + np.matmul(mix, z - 0.5)) + rng.integers(-6, 7, (N, 8, 16, L)), 0, 255).astype(np.int64)
    x = np.clip(np.rint(128 + np.matmul(mix, p - 0.5)) + rng.integers(-6, 7, (N, 8, 16, T * S)), 0, 255).astype(np.int64)
    ed = np.zeros((N, 8, 16, L), np.int64)
    for j in range(3):
        o = np.argsort(13 * np.floor(13 * z[:, :, j]) + np.floor(13 * z[:, :, (j + 1) % 3]) + z[:, :, (j + 2) % 3], axis=-1); at = np.argsort(o, axis=-1)
        for i in range(4): ed[:, :, 4 * j + i] = np.take_along_axis(o, (at + (1 - 2 * (i % 2)) * rng.integers(1, 7, (N, 8, L))) % L, -1)
    ids = ed[:, :, rng.permutation(12)]
    ed[:, :, :12] = np.where(rng.random(ids.shape) < 0.15, EMPTY, W * rng.integers(0, OLD + 1, ids.shape) + ids)
    ed[:, :, 12:] = (np.arange(L) + rng.integers(1, L, (N, 8, 4, L))) % L
    c = rng.integers(0, L, (N, 8, T * S, 8)); far = np.zeros(c.shape)
    for j in range(3): far = far + np.abs(np.take_along_axis(z[:, :, j], c.reshape(N, 8, -1), -1).reshape(c.shape) - p[:, :, j, :, None])
    best = np.take_along_axis(c, np.argmin(far, axis=-1)[..., None], -1)[..., 0]
    ent = np.where(rng.random(best.shape) < 0.5, best, c[..., 0])
    return w, ed, x, ent, rng.integers(100, 700, (N, 8))
def take(a, i): return np.take_along_axis(a, i[:, :, None, :], 3)
def pack(w, ed, x, ent, th):
    return {"w": np.ascontiguousarray(w.reshape(N, 128, L)).astype(np.float32).astype(BF), "nb": np.ascontiguousarray(ed.reshape(N, 128, L)).astype(np.int32),
            "x": np.ascontiguousarray(x.reshape(N, 128, T * S)).astype(np.float32).astype(BF), "ent": np.stack([gtable(a) for a in ent]),
            "th": np.repeat(th.reshape(N, 8, 1), 16, axis=2).reshape(N, 128, 1).astype(np.int32)}
def setup_inputs(rng):
    w, ed, x, ent, th = parts(rng); i = np.where(rng.random(ent.shape) < 0.15, rng.integers(0, T * S, ent.shape), np.arange(T * S))
    return pack(w, ed, take(x, i), np.take_along_axis(ent, i, -1), th)
def setup_inputs_crowd(rng):
    w, ed, x, ent, th = parts(rng); ent[..., 0] = 0; ent[..., 1] = L - 1
    pool = rng.choice(np.array([2, 5, 12, 40, 100, S, T * S]), (N, 8, 1)); pool[0, :, 0] = (1, 2, 3, 12, 40, 100, S, T * S)
    i = np.floor(rng.random(ent.shape) * pool).astype(np.int64)
    return pack(w, ed, take(x, i), np.take_along_axis(ent, i, -1), np.maximum(th - 80, 20))
def setup_inputs_room(rng):
    w, ed, x, ent, th = parts(rng); th[:] = 1; odd = np.add.reduce(w, axis=2) & 1; w[:, :, 0] = w[:, :, 0] ^ odd
    f = (0, C - 1, C, C + 1, C + X - 1, C + X, C + X + 1, S)
    for q in range(N):
        for g in range(8):
            o = rng.permutation(L); a, b = o[:S], o[S:2 * S]; n = f[g] if q == 0 else f[int(rng.integers(0, 8))]
            if n == 0 or n == S: w[q, g][:, a[-1]] = w[q, g][:, a[0]]; b[-1] = b[0]
            w[q, g][:, b] = w[q, g][:, a]; ed[q, g, 0, a] = W * rng.integers(0, OLD + 1, S) + b
            v = w[q, g][:, a]; v[3] = np.where(rng.permutation(S) < n, v[3] ^ 1, v[3])
            x[q, g, :, :S] = v; ent[q, g, :S] = a
    return pack(w, ed, x, ent, th)
def setup_inputs_ties(rng):
    w, ed, x, ent, th = parts(rng); point = rng.integers(0, 256, (N, 8, 16, 12)); point[:, :, 0] = rng.integers(0, 100, (N, 8, 12))
    w = take(point, rng.integers(0, 12, (N, 8, L))); th = rng.integers(3, 60, (N, 8))
    x = take(w, ent); x[:, :, 0] = x[:, :, 0] + th[..., None] + rng.integers(-1, 2, ent.shape)
    ent = np.where(rng.random(ent.shape) < 0.3, rng.integers(0, L, ent.shape), ent)
    h = ed[:, :, :6]; ed[:, :, 6:12] = np.where(h == EMPTY, EMPTY, W * rng.integers(0, OLD + 1, h.shape) + (h & (W - 1)))
    h = ed[:, 1::2, :12]; ed[:, 1::2, :12] = np.where(h == EMPTY, EMPTY, 4 * W + (h & (W - 1)))
    return pack(w, ed, x, ent, th)
def setup_inputs_aged(rng):
    w, ed, x, ent, th = parts(rng); x = np.tile(x[..., :S], (1, 1, 1, T)); ent = np.tile(ent[..., :S], (1, 1, T))
    th = np.where(rng.random((N, 8)) < 0.5, 4096, th)
    for q in range(N):
        for g in range(8):
            e = ed[q, g, :12]; ids = np.where(e == EMPTY, ed[q, g, 12:13], e & (W - 1)); age = rng.integers(0, OLD + 1, e.shape); i = (g + q) % 8
            if i < 3: e = np.where(e == EMPTY, EMPTY, (OLD - i) * W + ids)
            elif i == 3: e = np.full(e.shape, EMPTY)
            elif i == 4: e = age * W + ed[q, g, 12:13]
            elif i == 5: e = np.where(np.arange(12)[:, None] % 2 == 0, OLD, 0) * W + ids
            elif i == 6: e = 3 * (q % 2) * W + ids
            else: e = age * W + ids
            ed[q, g, :12] = e
    c = [int(i) for i in 1 + rng.permutation(L - 1)[:5]]; cut = [0] + c[2:]
    u = w[:, 1]; u[:, :, c + [0]] = 100; u[:, 1, c[1]] = 101
    for j in range(4): u[:, 0, cut[j]] = 140; u[:, 2 + j, cut[j]] = 160
    e = ed[:, 1]; e[:, :12, c[0]] = EMPTY; e[:, 0, c[0]] = c[1]
    for j in range(4): e[:, 12 + j, c[0]] = cut[j]
    x[:, 1] = 100; x[:, 1, 0, :S] = 180; x[:, 1, 0, S:] = 140
    for t in range(1, T): x[:, 1, 1 + t, t * S:(t + 1) * S] = 122
    ent[:, 1] = c[0]; th[:, 1] = 40
    return pack(w, ed, x, ent, th)
def setup_inputs_spread(rng):
    w, ed, x, ent, th = parts(rng)
    w = np.minimum(np.exp2(8.1 * rng.random((N, 8, 1, L))) * rng.random((N, 8, 16, L)), 255).astype(np.int64)
    x = np.minimum(np.exp2(8.1 * rng.random((N, 8, 1, T * S))) * rng.random((N, 8, 16, T * S)), 255).astype(np.int64)
    th = np.exp2(12 * rng.random((N, 8))).astype(np.int64); th[0, 0] = 0; th[1, 1] = 4096
    h = ed[:, ::2, :12]; ed[:, ::2, :12] = np.where(h == EMPTY, EMPTY, (h >> LG) * W + (np.arange(L) + rng.integers(1, L, h.shape)) % L)
    ent = np.where(rng.random(ent.shape) < 0.1, rng.choice(np.array([0, L - 1]), ent.shape), ent)
    for q in range(N):
        for g in (2, 3, 6, 7):
            w[q, g] = rng.integers(0, 4, (16, L)); x[q, g] = rng.integers(252, 256, (16, T * S))
            gone = rng.random((12, L)) < rng.choice(np.array([0.3, 0.6, 0.9, 1.0]), (1, L)); ed[q, g, :12] = np.where(gone, EMPTY, ed[q, g, :12])
            a, b = [int(c) for c in rng.permutation(L)[:2]]; i = (q + g) % 5; ent[q, g, 0] = a
            if i < 3:
                w[q, g, :, a] = 3; th[q, g] = np.add.reduce(x[q, g, :, 0]) - 48 + i - 1
            else:
                w[q, g, :, a] = 0; w[q, g, :, b] = 0; x[q, g, :, 0] = 255
                ed[q, g, :12, a] = EMPTY; ed[q, g, 12:, a] = b; th[q, g] = 4080 + i - 3
            if g >= 6: w[q, g] = 255 - w[q, g]; x[q, g] = 255 - x[q, g]
    return pack(w, ed, x, ent, th)
def check_inputs(d):
    bad = []
    for k in ("w", "x"):
        a = np.asarray(d[k]).astype(np.float32)
        if not np.all((a >= 0) & (a <= 255) & (a == np.floor(a))): bad.append("whole numbers of " + k)
    e = np.asarray(d["nb"]).astype(np.int64).reshape(N, 8, 16, L); own = np.arange(L); h = e[:, :, :12]; s = e[:, :, 12:]; c = h & (W - 1)
    if not np.all((h == EMPTY) | ((h >= 0) & (h < (OLD + 1) * W) & (c < L) & (c != own))): bad.append("edges of nb")
    if not np.all((s >= 0) & (s < L) & (s != own)): bad.append("shortcuts of nb")
    if np.min(d["ent"]) < 0 or np.max(d["ent"]) > L - 1: bad.append("range of ent")
    t = np.asarray(d["th"]).astype(np.int64).reshape(N, 8, 16)
    if np.min(t) < 0 or np.max(t) > 4096: bad.append("range of th")
    if not np.all(t == t[:, :, :1]): bad.append("th alike in a group")
    return bad
def near(wu, ed, xb, cur):
    a = np.arange(N * 8)[:, None]; c = ed[a, cur] & (W - 1)
    d = np.add.reduce(np.abs(xb[:, :, None, :] - wu[a[:, :, None], c]), axis=3)
    d = np.where(c == W - 1, 2 ** 20, d); i = np.argmin(d, axis=2)[:, :, None]
    return np.take_along_axis(c, i, 2)[:, :, 0], np.take_along_axis(d, i, 2)[:, :, 0]
def slot(e, c):
    return np.argmax(np.where((e[:, :12] & (W - 1)) == c[:, None], 16, e[:, :12] >> LG), axis=1)
def reference(w, nb, x, ent, th):
    M = N * 8; a = np.arange(M)[:, None]
    wu = np.zeros((M, W, 16), np.int32); wu[:, :L] = w.astype(np.float32).reshape(M, 16, L).transpose(0, 2, 1)
    ed = np.full((M, W, 16), EMPTY, np.int64); ed[:, :L] = nb.reshape(M, 16, L).transpose(0, 2, 1)
    xs = np.array(x.astype(np.float32).reshape(M, 16, T * S).transpose(0, 2, 1), dtype=np.int32, order="C")
    en = np.stack([gentries(b) for b in ent]).reshape(M, T * S).astype(np.int64)
    tv = th.astype(np.int64).reshape(M, 16)[:, :1]
    for t in range(T):
        xb = xs[:, t * S:(t + 1) * S]; eb = en[:, t * S:(t + 1) * S]; u = eb
        du = np.add.reduce(np.abs(xb - wu[a, u]), axis=2)
        for h in range(H):
            c, d = near(wu, ed, xb, u); go = d < du
            u = np.where(go, c, u); du = np.where(go, d, du)
        v, dv = near(wu, ed, xb, u)
        s = np.broadcast_to(np.arange(S), (M, S)); first = np.full((M, W), S)
        np.minimum.at(first, (a, u), s); np.minimum.at(first, (a, v), s)
        counts = (first[a, u] >= s) & (first[a, v] >= s)
        far = du >= tv; want = (counts & far).astype(np.int64); k = np.add.accumulate(want, axis=1) - want
        split = (want == 1) & (k < C); rest = far & ~split
        m, j = np.nonzero(counts); i = np.arange(len(m)); uu = u[m, j]; vv = v[m, j]; sp = split[m, j]; nn = L + C * t + k[m, j]
        xx = xb[m, j]; w0 = wu[m, uu]; w1 = wu[m, vv]; e0 = ed[m, uu]; e1 = ed[m, vv]; i0 = slot(e0, vv); i1 = slot(e1, uu)
        e0[:, :12] = np.where(e0[:, :12] + W >= (OLD + 1) * W, EMPTY, e0[:, :12] + W)
        e0[i, i0] = np.where(sp, nn, vv); e1[i, i1] = np.where(sp, nn, uu)
        e2 = np.full(e0.shape, EMPTY); e2[:, 0] = uu; e2[:, 1] = vv; e2[:, 12:] = e0[:, 12:]
        ed[m, uu] = e0; ed[m, vv] = e1; ed[m[sp], nn[sp]] = e2[sp]
        wu[m, uu] = w0 + ((xx - w0) >> 2); wu[m, vv] = w1 + ((xx - w1) >> 3); wu[m[sp], nn[sp]] = ((w0 + xx) >> 1)[sp]
        if t + 1 < T:
            place = np.argsort(~rest, axis=1, kind="stable")[:, :X]; num = np.add.reduce(rest.astype(np.int64), axis=1)
            kk = np.arange(X)[None, :]; q = (np.arange(N)[:, None] - 1 - kk % (N - 1)) % N
            mm = (q[:, None, :] * 8 + np.arange(8)[None, :, None]).reshape(M, X); pl = place[mm, kk]; got = num[mm] > kk
            lo, hi = (t + 2) * S - X, (t + 2) * S
            xs[:, lo:hi] = np.where(got[:, :, None], xb[mm, pl], xs[:, lo:hi]); en[:, lo:hi] = np.where(got, eb[mm, pl], en[:, lo:hi])
    P = L + T * C
    yw = np.ascontiguousarray(wu[:, :P].transpose(0, 2, 1)).reshape(N, 128, P).astype(np.float32).astype(BF)
    yn = np.ascontiguousarray(ed[:, :P].transpose(0, 2, 1)).reshape(N, 128, P).astype(np.float32)
    return {"yw": yw, "yn": yn}

@@ -1,0 +1,795 @@
+import math
+import numpy as np
+from concourse.bass import DstId, RemoteDMATransfer
+from concourse.mybir import AluOpType as ALU, ActivationFunctionType as AF
+
+L0, S, NT, HOPS, NEW, TRAVEL = 1152, 256, 3, 5, 32, 80
+OPT = dict(relu=True, nbs=(76, 76), chunk=2, arrive=6000.0, look=100.0, tol=70.0, boost=4000.0, hb=3000.0, nbby=3)
+COST = dict(gather=1.5, scatter=3.5, cyc=0.83, pe=0.42, sync=60.0, sfix=65.0)
+F32, BF, F16, I32, U16 = "float32", "bfloat16", "float16", "int32", "uint16"
+BIGK = float(2 ** 23)
+LNB, LNH = math.log(2.2), math.log(1.9)
+MAGIC = 1.5 * 2 ** 23
+
+SCRATCH = {}
+
+
+def sb(name, cols, dt):
+    SCRATCH[name] = ("sbuf", [128] + (list(cols) if isinstance(cols, tuple) else [cols]), dt)
+
+
+for n_, c_, d_ in [
+    ("W", 2048, F32), ("WB", 1248, BF), ("NBI", 1152, I32), ("IDI", 1152, I32), ("IDF", 1792, F32), ("NB", 1792, F32),
+    ("X", 768, BF), ("ENT", 48, I32), ("THI", 8, I32), ("XR0", 4096, BF), ("XR1", 4096, BF),
+    ("EL", 48, U16), ("EF", 48, F32), ("EH", 48, F16), ("CL", 16, U16), ("UVL", 32, U16), ("UVF", 32, F32),
+    ("VUH", 32, F16), ("CK5", 16, F32), ("FX", 256, BF), ("THX", 256, F32), ("COL", 48, F32), ("COI", 64, I32),
+    ("MAT", (17, 128), BF), ("M32", (4, 128), F32), ("SELT", (16, 128), BF), ("SEL", 144, BF), ("SEL2", 144, BF),
+    ("BC", 96, BF), ("WIDE", 240, BF), ("I17", 136, BF),
+    ("KC", (4, 136), BF), ("D0C", (2, 136), F32), ("DG", 32, F32), ("ZERO", 768, BF), ("IOF", 256, F32),
+    ("NOH", 1280, BF), ("ZT", 1280, BF), ("THR", 256, BF), ("DL", 32, F32), ("PERM", 12, U16), ("XL", 80, U16),
+    ("C1", 512, BF), ("C2", 512, BF), ("HALF", 512, BF), ("CW", 768, BF), ("C32", 256, BF), ("CN", 768, BF),
+    ("PKS0", 264, F32), ("PKS1", 264, F32), ("PKO", 160, F32), ("SND0", 80, F32), ("SND1", 80, F32),
+    ("LND0", 80, F32), ("LND1", 80, F32), ("NW", 80, F32), ("NWI", 240, I32), ("NWH", 80, F16),
+    ("THS", 512, BF), ("ZS", 512, BF), ("OH", (4, 128), BF), ("OL", (4, 8, 80), BF), ("FS", 640, F32), ("LOI", 32, I32),
+    ("LOL", 32, U16), ("BAD", 512, BF), ("WANT", 256, BF), ("P1C", 272, BF), ("PFAR", 256, BF), ("JUNK", 1792, BF),
+    ("RS", 8, F32), ("RL", 8, U16), ("OFT", 64, F32), ("OFL", 32, U16), ("TGS", 528, F32), ("TP", 512, F16),
+    ("TT", 520, F32), ("AG", 512, BF), ("EA", 512, BF), ("HH", 256, BF), ("MT", 512, BF), ("SG", 512, BF),
+    ("Z1", 512, F32), ("Z2", 512, F32), ("M1", 512, F32), ("M2", 512, F32), ("WUV", 512, BF), ("WR", 776, F32),
+    ("G1", 128, F32), ("G2", 136, F32),
+]:
+    sb(n_, c_, d_)
+for s_ in "AB":
+    for n_, c_, d_ in [("OFF", 128, U16), ("O16", 128, F16), ("EX", 128, F16), ("EB", 64, F16), ("DF", 2048, BF),
+                       ("WG", 2048, BF), ("AB", 2048, BF), ("S1", 136, F32), ("NQ", 136, BF), ("S2", 136, F32),
+                       ("D0", 136, F32), ("R8", 8, F32), ("CT", 8, F32), ("E0", 256, BF)]:
+        sb(n_ + s_, c_, d_)
+for n_ in ("P0", "P1", "P2", "P3", "P4", "P5", "P6"):
+    SCRATCH[n_] = ("psum", [128, 512], F32)
+SCRATCH["PB"] = ("psum", [128, 1024], BF)
+
+SEMAPHORES = ["sV", "sS", "sP", "sG", "arr0", "arr1", "rel0", "rel1", "sent"] + ["d%d" % i for i in range(12)]
+
+ALL = slice(None)
+
+
+def A(name, *idx):
+    return ("ap", name, idx)
+
+
+def C(name, a, b=None, step=None):
+    return A(name, slice(a, a + 1) if b is None else slice(a, b, step))
+
+
+def IND(win, off):
+    return ("ind", win, off)
+
+
+def is_ap(v):
+    return isinstance(v, tuple) and len(v) == 3 and v[0] in ("ap", "ind", "io")
+
+
+def res(T, v):
+    if not is_ap(v):
+        return v
+    if v[0] == "ind":
+        return res(T, v[1]).indirect(res(T, v[2]))
+    if v[0] == "io":
+        return T[v[1]][v[2]]
+    return T[v[1]][(ALL,) + v[2]]
+
+
+MASKS = {}
+
+
+def cols(v):
+    key = repr(v)
+    if key not in MASKS:
+        shape = SCRATCH[v[1]][1][1:]
+        c = np.arange(int(np.prod(shape))).reshape(shape)[v[2]].ravel()
+        m = 0
+        for i in c.tolist():
+            m |= 1 << i
+        MASKS[key] = (m, len(c))
+    return MASKS[key]
+
+
+def two(v):
+    return SCRATCH[v[1]][2] in (BF, F16, U16)
+
+
+def psum(v):
+    return SCRATCH[v[1]][0] == "psum"
+
+
+def build(t_ops):
+    GATHER, SCATTER, CYC, PECYC = COST["gather"], COST["scatter"], COST["cyc"], COST["pe"]
+
+    def op(e, fn, reads, writes, cost, lat=0.0, sem=None):
+        r, w = [], []
+        for v in reads:
+            if is_ap(v) and v[0] == "ind":
+                r += [v[1], v[2]]
+            elif is_ap(v) and v[0] == "ap":
+                r.append(v)
+        for v in writes:
+            if v[0] == "ind":
+                w.append(v[1]); r.append(v[2])
+            elif v[0] == "ap":
+                w.append(v)
+        t_ops.append(dict(e=e, fn=fn, r=r, w=w, cost=cost, lat=lat, sem=sem, after=[]))
+
+    def here():
+        return len(t_ops) - 1
+
+    def after(j):
+        t_ops[-1]["after"].append(j)
+
+    def vcost(out, ins, slow=False):
+        n = cols(ins[0])[1] if out[0] == "ind" else cols(out)[1]
+        if out[0] == "ind":
+            return 50 + n * SCATTER * CYC
+        if ins[0][0] == "ind":
+            return 50 + n * GATHER * CYC
+        f = 0.5 if two(out) and all(two(i) for i in ins) else 1.0
+        if slow:
+            f = 1.0 if any(psum(i) for i in ins) else 2.0
+        return max(64, n * f) * CYC + 10
+
+    def cp(out, in_):
+        op("V", lambda g, T: g.vector.tensor_copy(res(T, out), res(T, in_)), [in_], [out], vcost(out, [in_]))
+
+    def tt(out, a, b, o):
+        op("V", lambda g, T: g.vector.tensor_tensor(res(T, out), res(T, a), res(T, b), o), [a, b], [out],
+           vcost(out, [a, b], True))
+
+    def ts(out, a, s1, o0, s2=None, o1=None):
+        def fn(g, T):
+            if o1 is None:
+                return g.vector.tensor_scalar(res(T, out), res(T, a), res(T, s1), None, o0)
+            return g.vector.tensor_scalar(res(T, out), res(T, a), res(T, s1), res(T, s2), o0, o1)
+        op("V", fn, [a, s1, s2], [out], vcost(out, [a]))
+
+    def scan(out, d0, d1, o0, o1):
+        op("V", lambda g, T: g.vector.tensor_tensor_scan(res(T, out), res(T, d0), res(T, d1), 0.0, o0, o1), [d0, d1], [out],
+           vcost(out, [d0, d1]))
+
+    def ms(out, val):
+        op("V", lambda g, T: g.vector.memset(res(T, out), val), [], [out], vcost(out, [out]))
+
+    def act(out, in_, f, bias=0.0, scale=1.0, acc=None, extra=0.0):
+        n = cols(out)[1]
+        c = COST["sfix"] + extra + n * CYC * (GATHER if in_[0] == "ind" else 1.0)
+        op("S", lambda g, T: g.scalar.activation(res(T, out), res(T, in_), f, bias=res(T, bias), scale=res(T, scale),
+                                                 accum_out=res(T, acc)),
+           [in_, bias, scale], [out] + ([acc] if acc else []), c)
+
+    def mm(out, lhsT, rhs, start, stop):
+        c = max(64, cols(rhs)[1]) * PECYC * (1 if two(rhs) else 4)
+        op("P", lambda g, T: g.tensor.matmul(res(T, out), res(T, lhsT), res(T, rhs), start, stop), [lhsT, rhs], [out], c, 60)
+
+    def group(items):
+        for i, (o, l, r) in enumerate(items):
+            mm(o, l, r, i == 0, i == len(items) - 1)
+
+    def ptr(out, in_, ident):
+        op("P", lambda g, T: g.tensor.transpose(res(T, out), res(T, in_), res(T, ident)), [in_, ident], [out], 128 * PECYC, 60)
+
+    def iota(out, pat, base, cm):
+        flag = SCRATCH[out[1]][2] != I32
+
+        def fn(g, T):
+            if flag:
+                return g.iota(res(T, out), pat, base, cm, allow_small_or_imprecise_dtypes=True)
+            return g.iota(res(T, out), pat, base, cm)
+        op("G", fn, [], [out], 130 + 2 * CYC * cols(out)[1])
+
+    def aff(out, in_, pat, cmp_, fill, base, cm):
+        op("G", lambda g, T: g.affine_select(res(T, out), res(T, in_), pat, cmp_, fill, base, cm), [in_], [out],
+           170 + 2 * CYC * cols(out)[1])
+
+    def gcopy(out, in_):
+        aff(out, in_, [[0, cols(out)[1]]], ALU.is_ge, 0.0, 0, 0)
+
+    def gfill(out, val):
+        n = cols(out)[1]
+        aff(out, C("ZERO", 0, n), [[0, n]], ALU.is_gt, val, 0, 0)
+
+    nd = [0]
+
+    def dma(q, out, in_, lat):
+        sem = "d%d" % nd[0]; nd[0] += 1
+        if q == "Y":
+            op("Y", lambda g, T: g.sync.dma_start(res(T, out), res(T, in_)), [in_], [out], 60, lat, sem)
+        else:
+            op("S", lambda g, T: g.scalar.dma_start(res(T, out), res(T, in_)), [in_], [out], 60, lat, sem)
+
+    ID, NID, BO, NBO, LA, LT, I75, I25, I875, I125, I50, I256, IB, NIB, I2K, NI2K, DGM = [A("MAT", i) for i in range(17)]
+    I32M, NI32M, ONE32, THB = [A("M32", i) for i in range(4)]
+    BC1, BC128, NBC64, BMR = C("BC", 0, 8), C("BC", 8, 16), C("BC", 16, 24), C("BC", 32, 96)
+    L8 = C("PERM", 6, 10)
+    relu = OPT["relu"]
+    prev = {"NB": []}
+
+    def sel(a, name="SEL"):
+        return C(name, 15 - a, 143 - a)
+
+    dma("Y", C("X", 0, 256), ("io", "x", (ALL, slice(0, 256))), 2000)
+    dma("S", A("ENT"), ("io", "ent", (ALL,)), 2000)
+    dma("Y", A("NBI"), ("io", "nb", (ALL,)), 3200)
+    dma("S", C("WB", 0, L0), ("io", "w", (ALL,)), 2600)
+    dma("Y", C("X", 256, 768), ("io", "x", (ALL, slice(256, 768))), 3600)
+    dma("Y", C("THI", 0), ("io", "th", (ALL,)), 2500)
+
+    ms(A("ZERO"), 0.0)
+    ms(C("W", L0, 2047), 0.0); ms(C("W", 2047), 512.0)
+    Z128 = C("ZERO", 0, 128)
+
+    def diag(out, val):
+        aff(out, Z128, [[-1, 128]], ALU.not_equal, val, 0, 1)
+    diag(ID, 1.0); diag(NID, -1.0); diag(I32M, 1.0)
+    iota(C("COI", 0), [[0, 1]], 0, 1)
+    ts(C("COI", 1), C("COI", 0), 15, ALU.bitwise_and)
+    ts(C("COI", 2), C("COI", 0), 4, ALU.logical_shift_right)
+    cI, cG = C("COL", 1), C("COL", 2)
+    cp(C("COL", 1, 3), C("COI", 1, 3))
+    iota(C("G1", 0, 128), [[0, 8], [1, 16]], 0, 0)
+    ts(DGM, C("G1", 0, 128), cI, ALU.is_equal)
+    ts(C("DG", 0, 16), C("G1", 0, 16), cI, ALU.is_equal)
+    iota(C("G2", 0, 80), [[1, 80]], 0, 0)
+    cp(A("XL"), C("G2", 0, 80))
+    cp(C("COL", 32, 40), C("G2", 0, 8))
+    ts(BC1, C("COL", 32, 40), cG, ALU.is_equal)
+    ms(A("WIDE"), 0.0); cp(C("WIDE", 112, 128), C("DG", 0, 16))
+    iota(C("G2", 128, 132), [[2, 4]], 0, 0)
+    ts(C("COL", 3), cI, 8.0, ALU.is_ge)
+    ts(L8, C("G2", 128, 132), C("COL", 3), ALU.add)
+    iota(C("THX", 0, 64), [[0, 8], [1, 8]], 0, 0)
+    ts(BMR, C("THX", 0, 64), cG, ALU.is_equal)
+    ts(BC128, BC1, 128.0, ALU.mult); ts(NBC64, BC1, -64.0, ALU.mult)
+    aff(A("I17"), C("ZERO", 0, 136), [[16, 8], [1, 17]], ALU.not_equal, 1.0, -1, -1)
+    ms(C("I17", 0, 136, 17), 0.0)
+    iota(A("KC", 1), [[0, 8], [1, 17]], 0, 0)
+    iota(C("IOF", 0, 136), [[1, 8], [0, 17]], 0, 0)
+    ts(A("KC", 0), C("IOF", 0, 136), float(2 ** 19), ALU.mult)
+    cp(A("KC", 2), A("KC", 0)); ms(A("KC", 2, slice(0, 136, 17)), BIGK)
+    iota(C("FS", 0, 136), [[32, 8], [-1, 17]], 16, 0)
+    ts(A("KC", 3), C("FS", 0, 136), 4096.0, ALU.mult)
+    ms(A("D0C"), 0.0); ms(A("D0C", 0, slice(0, 136, 17)), BIGK)
+    ts(A("D0C", 1, slice(0, 136, 17)), C("IOF", 0, 136, 17), float(2 ** 19), ALU.mult, 64.0 * 4090, ALU.add)
+    ms(A("D0A"), 0.0); ms(A("D0B"), 0.0)
+    if relu:
+        for s in range(2):
+            ms(C("DF" + "AB"[s], 0, 16 * OPT["nbs"][s]), 0.0)
+
+    cp(A("EL"), A("ENT")); cp(A("EF"), A("ENT"))
+    for i in range(16):
+        cp(C("XR0", i, 2048, 16), C("X", 0, 128))
+    for i in range(16):
+        if i < 8:
+            act(C("XR0", 2048 + i, 4096, 16), C("X", 128, 256), AF.Copy)
+        else:
+            cp(C("XR0", 2048 + i, 4096, 16), C("X", 128, 256))
+    act(C("W", 0, L0), C("WB", 0, L0), AF.Copy)
+    ts(A("IDI"), A("NBI"), 2047, ALU.bitwise_and)
+    gcopy(C("IDF", 0, L0), A("IDI"))
+    gfill(C("IDF", L0, 1792), 2047.0)
+
+    def late_setup():
+        gcopy(C("NB", 0, L0), A("NBI")); gfill(C("NB", L0, 1792), 32767.0)
+        for m, v in [(I75, .75), (I25, .25), (I875, .875), (I125, .125), (I50, .5), (I256, 1 / 256), (IB, 32768.0),
+                     (NIB, -32768.0), (I2K, 2048.0), (NI2K, -2048.0), (NI32M, -1.0)]:
+            diag(m, v)
+        gfill(ONE32, 1.0)
+        aff(BO, ONE32, [[-16, 8], [0, 16]], ALU.is_ge, 0.0, 0, 1)
+        aff(BO, BO, [[16, 8], [0, 16]], ALU.is_ge, 0.0, 15, -1)
+        ts(NBO, BO, -1.0, ALU.mult)
+        gfill(A("SEL"), 0.0); gfill(A("SEL2"), 0.0)
+        ts(C("SEL", 15, 143, 16), BC1, 64.0, ALU.mult)
+        ts(C("SEL2", 15, 143, 16), BC1, 2048.0, ALU.mult)
+        for a in range(16):
+            ts(A("SELT", a), BO, C("DG", a), ALU.mult)
+        ts(C("COL", 5), cI, 12.0, ALU.is_lt)
+        ts(C("COL", 6), cI, -LNB, ALU.mult, 11 * LNB - 80, ALU.add)
+        act(C("COL", 7), C("COL", 6), AF.Exp, bias=192 * LNB, extra=1300)
+        prev["exp"] = here()
+        aff(LA, BO, [[-1, 128]], ALU.not_equal, -1.0, 0, 1)
+        ts(LA, LA, C("COL", 5), ALU.mult)
+        ts(LT, LA, C("COL", 7), ALU.mult)
+        ts(C("COL", 8), cI, 12.0, ALU.is_ge)
+        ts(C("COL", 9), cI, 2.0, ALU.is_ge, C("COL", 5), ALU.mult)
+        ts(C("COL", 9), C("COL", 9), 32767.0, ALU.mult)
+        ts(C("COL", 10), cG, 80.0, ALU.mult, -0.46875, ALU.add)
+        ts(C("COL", 11), C("COL", 5), -2048.0, ALU.mult, -1024.0, ALU.add)
+        ts(C("C1", 0, 256), C("ZERO", 0, 256), C("COL", 11), ALU.add)
+        gfill(C("C1", 256, 512), -1024.0); gfill(A("C2"), -31744.0); gfill(A("HALF"), -0.5)
+        gfill(C("CW", 0, 256), -0.375); gfill(C("CW", 256, 512), -0.4375); gfill(C("CW", 512, 768), -0.25)
+        gfill(A("C32"), 32.0)
+        for t in range(NT):
+            gfill(C("CN", 256 * t, 256 * t + 256), -896.0 + 32 * t)
+        gfill(C("P1C", 0, 16), 0.0)
+        gfill(C("TT", 256, 264), 32767 - 1023.5); gfill(C("TGS", 256, 264), 32767.0); gfill(C("TGS", 520, 528), 32767.0)
+        gfill(C("WR", 768, 776), MAGIC)
+        gfill(C("PKS0", 256, 264), 0.0); gfill(C("PKS1", 256, 264), 0.0)
+        iota(A("IOF"), [[1, 256]], 0, 0)
+        act(A("THR"), A("IOF"), AF.Exp, bias=80 + math.log(2.5), scale=-LNH)
+        iota(C("COL", 14, 16), [[128, 2]], 0, 1)
+        act(C("COL", 12, 14), C("COL", 14, 16), AF.Exp, bias=80.0, scale=-LNH)
+        ts(C("DG", 16, 32), C("DG", 0, 16), -1.0, ALU.mult, 1.0, ALU.add)
+        ts(C("NOH", 0, 16), C("DG", 16, 32), float(2 ** 62), ALU.mult, float(2 ** 62), ALU.mult)
+        n = 16
+        while n < 1280:
+            m = min(n, 1280 - n)
+            gcopy(C("NOH", n, n + m), C("NOH", 0, m)); n += m
+        for i in range(16):
+            gcopy(C("ZT", i, 256, 16), C("DG", 0, 16))
+        for k in range(1, 5):
+            ts(C("ZT", 256 * k, 256 * k + 256), C("ZT", 0, 256), float(k + 1), ALU.mult)
+        iota(C("G2", 96, 128), [[16, 32]], 1280, 0)
+        ts(A("DL"), C("G2", 96, 128), cI, ALU.add)
+        ts(C("COL", 40), cI, 5.0, ALU.mult, 0.5, ALU.add)
+        ts(C("COL", 16, 21), C("COL", 32, 37), C("COL", 40), ALU.add)
+        ts(C("COL", 41), cI, 0.5, ALU.add)
+        ts(C("COL", 22, 24), C("COL", 32, 34), 16.0, ALU.mult, C("COL", 41), ALU.add)
+        ts(C("COL", 24, 30), C("COL", 32, 38), 16.0, ALU.mult, cI, ALU.add)
+        ts(C("COI", 8, 14), C("COL", 24, 30), -2.0, ALU.add, 0.2, ALU.mult)
+        ts(C("COL", 42, 48), C("COI", 8, 14), -79.0, ALU.mult)
+        ts(C("COL", 24, 30), C("COL", 24, 30), 16.0, ALU.mult)
+        tt(C("COL", 42, 48), C("COL", 42, 48), C("COL", 24, 30), ALU.add)
+        cp(C("PERM", 0, 6), C("COL", 42, 48))
+        cp(C("COL", 30), C("THI", 0))
+        ts(THB, BO, C("COL", 30), ALU.mult, 4.0, ALU.mult)
+        mm(C("P6", 0, 128), ONE32, THB, True, True)
+        iota(C("THX", 128, 256), [[1, 8], [0, 16]], 0, 0)
+        ts(C("THX", 128, 256), C("THX", 128, 256), float(2 ** 19), ALU.mult)
+        tt(C("THX", 0, 128), C("THX", 128, 256), C("P6", 0, 128), ALU.add)
+        cp(A("EH"), A("ENT"))
+        group([(A("P6"), I256, C("X", 0, 512))] + [(C("P6", a, 512, 16), A("SELT", a), C("EH", 0, 32)) for a in range(16)])
+        act(C("PKS0", 0, 256), C("P6", 0, 256), AF.Identity, bias=float(2 ** 19), scale=256.0)
+        act(C("PKS1", 0, 176), C("P6", 256, 432), AF.Identity, bias=float(2 ** 19), scale=256.0)
+        act(C("PKO", 0, 80), C("P6", 432, 512), AF.Identity, scale=256.0)
+        group([(C("P6", 0, 80), I256, C("X", 688, 768))] +
+              [(C("P6", a, 80, 16), A("SELT", a), C("EH", 43, 48)) for a in range(16)])
+        act(C("PKO", 80, 160), C("P6", 0, 80), AF.Identity, scale=256.0)
+
+    def near(t, h, s):
+        n = "AB"[s]; K = "P%d" % s; banks = ("P2", "P3") if s == 0 else ("P4", "P5")
+        XR = "XR%d" % (t % 2); x0 = 2048 * s; lo = 8 * s
+        if h == 0:
+            lst = C("EL", 16 * t + lo, 16 * t + lo + 8)
+        else:
+            lst = C("UVL" if h == HOPS else "CL", lo, lo + 8)
+        ids = A("IDI") if t == 0 and h == 0 else A("IDF")
+        cp(A("O16" + n), IND(ids, lst))
+        if 2 * h + s >= OPT["nbby"] and prev["NB"]:
+            after(prev["NB"].pop(0))
+        if t == 0 and 2 * h + s == 2:
+            after(prev["exp"])
+        cp(A("OFF" + n), A("O16" + n))
+        nb = OPT["nbs"][s]
+        parts = [(b, min(nb, b + 32)) for b in range(0, nb, 32)]
+        for b, e in parts:
+            act(C("WG" + n, 16 * b, 16 * e), IND(A("W"), C("OFF" + n, b, e)), AF.Copy)
+            if b == 0 and "S" in prev:
+                after(prev["S"])
+        k = OPT["chunk"]
+        cut = [nb + 2 * (((128 - nb) // 2 * i) // k) for i in range(k + 1)]
+        for b, e in zip(cut, cut[1:]):
+            d, ab = C("DF" + n, 16 * b, 16 * e), C("AB" + n, 16 * b, 16 * e)
+            tt(d, IND(A("W"), C("OFF" + n, b, e)), C(XR, x0 + 16 * b, x0 + 16 * e), ALU.subtract)
+            if b == nb and "V" in prev:
+                after(prev["V"])
+            prev["V"] = here()
+            if relu:
+                ts(ab, d, 0.0, ALU.max)
+            else:
+                act(ab, d, AF.Abs, scale=0.5)
+        key, idt = C(K, 0, 136), C(K, 136, 272)
+        items = [(idt, ID, A("KC", 3)), (idt, A("O16" + n), A("I17"))]
+        if h == 0:
+            tt(C("E0" + n, 0, 128), IND(A("W"), lst), C("X", 256 * t + 128 * s, 256 * t + 128 * s + 128), ALU.subtract)
+            act(C("E0" + n, 128, 256), C("E0" + n, 0, 128), AF.Abs, scale=0.5)
+            tt(A("EX" + n), IND(C("EF", 16 * t + lo, 16 * t + lo + 8), C("XL", 0, 8)), DGM, ALU.mult)
+            items.append((C(K, 136, 272, 17), A("EX" + n), BC1))
+        elif h < HOPS:
+            items.append((C(K, 136, 272, 17), I32M, A("CT" + n)))
+        group(items)
+        for k, (b, e) in enumerate(parts):
+            o = C(banks[k % 2], 0, 16 * (e - b))
+            group([(o, NID, C(XR, x0 + 16 * b, x0 + 16 * e)), (o, ID, C("WG" + n, 16 * b, 16 * e))])
+            act(C("AB" + n, 16 * b, 16 * e), o, AF.Abs, scale=0.5)
+            prev["S"] = here()
+        items = [(key, ID, A("KC", 0 if h == 0 else 2)), (key, ID, A("KC", 1))]
+        if h == 0:
+            items.append((C(K, 0, 136, 17), C("E0" + n, 128, 256), BC128))
+        if relu:
+            items += [(C(K, 1 + i, 136, 17), C("DF" + n, i, 2048, 16), NBC64) for i in range(16)]
+        items += [(C(K, 1 + i, 136, 17), C("AB" + n, i, 2048, 16), BC128) for i in range(16)]
+        group(items)
+        d0 = A("D0C", 0) if h == 0 else A("D0C", 1) if h == HOPS else A("D0" + n)
+        scan(A("S1" + n), d0, key, ALU.max, ALU.min)
+        tt(A("NQ" + n), A("S1" + n), key, ALU.not_equal)
+        scan(A("S2" + n), A("NQ" + n), idt, ALU.mult, ALU.max)
+        last = C("S2" + n, 16, 136, 17)
+        ts(A("R8" + n), last, 1.5 * 2 ** 35, ALU.add, 1.5 * 2 ** 35, ALU.subtract)
+        tt(A("CT" + n), last, A("R8" + n), ALU.subtract)
+        tt(A("EB" + n), IND(A("CT" + n), L8), BMR, ALU.mult)
+        lp = C(K, 272, 280)
+        group([(lp, C("WIDE", 112 - 16 * k, 240 - 16 * k), C("EB" + n, 8 * k, 8 * k + 8)) for k in range(8)])
+        if h < HOPS - 1:
+            cp(C("CL", lo, lo + 8), lp)
+        else:
+            q = h - HOPS + 1
+            cp(C("UVL", 16 * q + lo, 16 * q + lo + 8), lp)
+            cp(C("UVF", 16 * q + lo, 16 * q + lo + 8), lp)
+            cp(C("VUH", 16 - 16 * q + lo, 24 - 16 * q + lo), lp)
+        if h < HOPS:
+            o = C("D0" + n, 0, 136, 17) if h < HOPS - 1 else C("CK5", lo, lo + 8)
+            ts(o, C("S1" + n, 16, 136, 17), 1.5 * 2 ** 29, ALU.add, 1.5 * 2 ** 29, ALU.subtract)
+
+    def item(t, q):
+        lst = C("UVL", 16 * q, 16 * q + 16); a, b = 256 * q, 256 * q + 256
+        act(C("ZS", a, b), IND(A("ZT"), lst), AF.Copy)
+        tt(C("THS", a, b), IND(A("NOH"), lst), A("THR"), ALU.max)
+        ts(C("LOI", 16 * q, 16 * q + 16), C("UVF", 16 * q, 16 * q + 16), 1 / 16, ALU.mult, C("COL", 10), ALU.add)
+        cp(C("LOL", 16 * q, 16 * q + 16), C("LOI", 16 * q, 16 * q + 16))
+        for h in range(2):
+            ptr(C("PB", a + 128 * h, a + 128 * h + 128), C("ZS", a + 128 * h, a + 128 * h + 128), ID)
+        for h in range(2):
+            mm(C("P6", 128 * h, 128 * h + 128), C("THS", a + 128 * h, a + 128 * h + 128), ID, True, True)
+        act(A("OH", slice(2 * q, 2 * q + 2)), C("P6", 0, 256), AF.Relu, bias=1.0, scale=-2.0 ** -124)
+        for h in range(2):
+            for k in range(5):
+                ts(A("OL", 2 * q + h, ALL, slice(16 * k, 16 * k + 16)), C("PB", a + 128 * h, a + 128 * h + 128),
+                   float(k + 1), ALU.is_equal, C("COL", 12 + h), ALU.mult)
+        c = 264 * q
+        act(C("TT", c, c + 256), IND(A("NB"), lst), AF.Identity, bias=-1023.5)
+        ts(C("AG", a, b), C("TT", c, c + 256), 1.5 * 2 ** 34, ALU.add, 1.5 * 2 ** 34, ALU.subtract)
+        act(C("EA", a, b), C("AG", a, b), AF.Exp, bias=C("COL", 6), scale=12 * LNB / 2048)
+        if q == 0:
+            act(A("HH"), C("AG", 0, 256), AF.Relu, bias=-245760.0, scale=16.0)
+        act(C("WUV", a, b), IND(A("W"), lst), AF.Copy)
+        x = C("X", 256 * t, 256 * t + 256)
+        o = C("P4" if q else "P6", 256, 512)
+        group([(o, ID, C("CW", a, b)), (o, I125 if q else I25, x), (o, I875 if q else I75, C("WUV", a, b))])
+        act(C("WR", a, b), o, AF.Identity, bias=MAGIC)
+        k = "P5" if q else "P6"
+        group([(C(k, i, 256, 16), A("SELT", i), C("VUH", 16 - 16 * q, 32 - 16 * q)) for i in range(16)])
+        act(C("TGS", 264 - c, 520 - c), C(k, 0, 256), AF.Copy)
+        if q == 0:
+            group([(o, ID, C("CW", 512, 768)), (o, I50, x), (o, I50, C("WUV", 0, 256))])
+            act(C("WR", 512, 768), o, AF.Identity, bias=MAGIC)
+
+    def far_mm(c):
+        return [(C("P6", c + 128 * s, c + 128 * s + 128), C("FX", 128 * s, 128 * s + 128), ID) for s in range(2)]
+
+    def far(t):
+        for s in range(2):
+            tt(C("FX", 128 * s, 128 * s + 128), IND(C("CK5", 8 * s, 8 * s + 8), C("XL", 0, 8)), C("THX", 0, 128), ALU.is_ge)
+        if t < NT - 1:
+            group(far_mm(256))
+            scan(A("PFAR"), C("P6", 256, 512), C("ZERO", 0, 256), ALU.add, ALU.add)
+
+    def edits(t):
+        last = t == NT - 1
+        for k in range(2):
+            group([(C("P%d" % (2 + k), 0, 320), A("OH", j), A("OL", j, slice(4 * k, 4 * k + 4))) for j in range(4)])
+        act(C("FS", 0, 320), C("P2", 0, 320), AF.Copy)
+        cp(C("FS", 320, 640), C("P3", 0, 320))
+        for q in range(2):
+            tt(C("BAD", 256 * q, 256 * q + 256), IND(A("FS"), C("LOL", 16 * q, 16 * q + 16)), C("THS", 256 * q, 256 * q + 256),
+               ALU.is_gt)
+        group(far_mm(0) + [(C("P6", 0, 256), NBO, C("BAD", 256 * q, 256 * q + 256)) for q in range(2)])
+        group([(C("P1", 0, 16), sel(a, "SEL2"), C("BAD", 256 * q + a, 256 * q + 256, 16)) for q in range(2) for a in range(16)])
+        ts(A("WANT"), C("P6", 0, 256), 1.0, ALU.is_equal)
+        p_now, p_prev = C("P1C", 16, 272), C("P1C", 15, 271)
+        scan(p_now, A("WANT"), A("C32"), ALU.add, ALU.min)
+        if not last:
+            group([(C("P0", 0, 256), ID, A("PFAR")), (C("P0", 0, 256), NID, p_now)])
+            for j in range(5):
+                act(C("JUNK", 256 * j, 256 * j + 256), C("P0", 0, 256), AF.Sign, bias=C("COL", 16 + j), scale=-1.0,
+                    acc=C("RS", j))
+            ts(C("RL", 0, 5), C("RS", 0, 5), 0.5, ALU.mult, 128.0, ALU.add)
+            cp(A("SND%d" % t), IND(A("PKS%d" % t), C("RL", 0, 5)))
+            op("G", ("send", t), [A("SND%d" % t)], [], 1500, 0, "none")
+        for q in range(2):
+            tt(C("OFT", 16 * q, 16 * q + 16), C("UVF", 16 * q, 16 * q + 16), C("P1", 0, 16), ALU.add)
+        tt(C("OFT", 32, 64), C("OFT", 0, 32), A("DL"), ALU.min)
+        cp(A("OFL"), C("OFT", 32, 64))
+        for q in range(2):
+            tt(C("MT", 256 * q, 256 * q + 256), IND(A("IDF"), C("UVL", 16 * q, 16 * q + 16)), C("TGS", 264 * q, 264 * q + 256),
+               ALU.is_equal)
+        group([(A("P5"), LA, A("EA")), (A("P5"), LT, A("MT"))])
+        act(A("SG"), A("P5"), AF.Sign)
+        group([(C("P6", 0, 256), ID, C("CN", 256 * t, 256 * t + 256)), (C("P6", 0, 256), I2K, p_now),
+               (C("P6", 0, 256), NI2K, p_prev), (C("P6", 0, 256), ID, p_prev)])
+        for q in range(2):
+            tt(C("TP", 256 * q, 256 * q + 256), C("TGS", 264 * q, 264 * q + 256), C("P6", 0, 256), ALU.max)
+        group([(A("P5"), NIB, A("SG")), (A("P5"), NID, A("TP"))])
+        ts(IND(C("W", 0, 1792), A("OFL")), C("WR", 0, 512), 1.0, ALU.mult, -MAGIC, ALU.add)
+        wsc = here()
+
+        def lin(bank, const, age):
+            items = [(A(bank), ID, const), (A(bank), ID, A("HALF")), (C(bank, 0, 256), NID, A("HH"))]
+            items += [(C(bank, 256 * q, 256 * q + 256), NI32M, C("TT", 264 * q, 264 * q + 256)) for q in range(2)]
+            if age:
+                items.append((A(bank), ID, A("AG")))
+            group(items + [(A(bank), IB, A("SG"))])
+        if not last:
+            lin("P3", A("C2"), True)
+            act(A("Z2"), A("P5"), AF.Relu, bias=-30721.0)
+            tt(A("M2"), A("Z2"), A("P3"), ALU.max)
+            ts(IND(A("IDF"), A("OFL")), A("M2"), -1.0, ALU.mult, 2047.0, ALU.add)
+            after(wsc)
+        lin("P2", A("C1"), False)
+        act(A("Z1"), A("P5"), AF.Relu, bias=-1.0)
+        tt(A("M1"), A("Z1"), A("P2"), ALU.max)
+        for j in range(2):
+            act(C("JUNK", 1280 + 256 * j, 1536 + 256 * j), p_now, AF.Sign, bias=C("COL", 22 + j), scale=-1.0, acc=C("RS", 6 + j))
+        sl = C("RL", 6, 8)
+        ts(sl, C("RS", 6, 8), 0.5, ALU.mult, 128.0, ALU.add)
+        c = L0 + NEW * t
+        ts(C("W", c, c + NEW), IND(C("WR", 512, 776), sl), -MAGIC, ALU.add)
+        ts(C("G1", 0, 32), IND(C("TT", 0, 264), sl), 1023.5, ALU.add, C("COL", 8), ALU.mult)
+        ts(C("G1", 32, 64), IND(C("TGS", 0, 264), sl), C("DG", 1), ALU.mult, C("COL", 9), ALU.add)
+        ts(C("G1", 64, 96), IND(C("TGS", 264, 528), sl), C("DG", 0), ALU.mult)
+        tt(C("G1", 96, 128), C("G1", 0, 32), C("G1", 32, 64), ALU.add)
+        tt(C("G1", 0, 32), C("G1", 96, 128), C("G1", 64, 96), ALU.add)
+        if not last:
+            ts(C("IDF", c, c + NEW), C("G1", 0, 32), 2047.0, ALU.min)
+        cp(C("NB", c, c + NEW), C("G1", 0, 32))
+        k = 1 if last else 4
+        for j in range(k):
+            ts(IND(A("NB"), C("OFL", 32 * j // k, 32 * (j + 1) // k)), C("M1", 512 * j // k, 512 * (j + 1) // k),
+               -1.0, ALU.mult, 32767.0, ALU.add)
+            prev["NB"].append(here())
+        if last:
+            after(wsc)
+
+    def arrive(t):
+        e = t - 1; c = 256 * t + 176
+        op("R", ("arrive", e), [A("SND%d" % e)], [A("LND%d" % e)], 0, OPT["arrive"], "arr%d" % e)
+        tt(A("NW"), IND(A("LND%d" % e), C("PERM", 0, 5)), C("PKO", 80 * e, 80 * e + 80), ALU.max)
+        cp(C("NWI", 0, 80), A("NW"))
+        ts(C("NWI", 160, 240), C("NWI", 0, 80), 255, ALU.bitwise_and)
+        cp(C("X", c, c + 80), C("NWI", 160, 240))
+        ts(C("NWI", 80, 160), C("NWI", 0, 80), 8, ALU.logical_shift_right, 2047, ALU.bitwise_and)
+        cp(A("NWH"), C("NWI", 80, 160))
+        group([(C("P6", 0, 5), sel(a), C("NWH", a, 80, 16)) for a in range(16)])
+        ts(C("EL", 16 * t + 11, 16 * t + 16), C("P6", 0, 5), 1 / 1024, ALU.mult)
+        ts(C("EF", 16 * t + 11, 16 * t + 16), C("P6", 0, 5), 1 / 1024, ALU.mult)
+        XR = "XR%d" % (t % 2)
+        act(C(XR, 2816, 3456), IND(C("X", c, c + 80), C("XL", 0, 40)), AF.Copy)
+        cp(C(XR, 3456, 4096), IND(C("X", c, c + 80), C("XL", 40, 80)))
+        if t < NT - 1:
+            ts(C("PKS%d" % t, 176, 256), A("NW"), float(2 ** 19), ALU.add)
+
+    for t in range(NT):
+        for h in range(HOPS + 1):
+            if h == HOPS:
+                far(t); item(t, 0)
+            near(t, h, 0)
+            if h == 0 and t > 0:
+                arrive(t)
+            near(t, h, 1)
+            if h == 0:
+                if t == 0:
+                    late_setup()
+                if t + 1 < NT:
+                    for i in range(16):
+                        gcopy(C("XR%d" % ((t + 1) % 2), i, 2816, 16), C("X", 256 * t + 256, 256 * t + 432))
+        item(t, 1)
+        edits(t)
+    act(A("WB"), C("W", 0, 1248), AF.Copy)
+    dma("S", ("io", "yw", (ALL,)), A("WB"), 2500)
+    dma("Y", ("io", "yn", (ALL,)), C("NB", 0, 1248), 3000)
+
+
+def plan():
+    ops = []
+    build(ops)
+    n = len(ops)
+    SYNC = COST["sync"]
+    wr, rd, bank = {}, {}, {}
+    deps = []
+    for i, o in enumerate(ops):
+        d = {}
+        for v in o["r"]:
+            m = cols(v)[0]
+            for j, mj in wr.get(v[1], []):
+                if mj & m:
+                    d[j] = True
+        for v in o["w"]:
+            m = cols(v)[0]
+            for j, mj in wr.get(v[1], []) + rd.get(v[1], []):
+                if mj & m and j != i:
+                    d[j] = True
+        for v in o["r"] + o["w"]:
+            if psum(v):
+                for j in bank.get(v[1], {}).values():
+                    if j != i:
+                        d.setdefault(j, False)
+        for v in o["r"]:
+            rd.setdefault(v[1], []).append((i, cols(v)[0]))
+        for v in o["w"]:
+            m = cols(v)[0]
+            wr[v[1]] = [(j, mj) for j, mj in wr.get(v[1], []) if mj & ~m] + [(i, m)]
+            rd[v[1]] = [(j, mj) for j, mj in rd.get(v[1], []) if mj & ~m or j == i]
+        for v in o["r"] + o["w"]:
+            if psum(v):
+                bank.setdefault(v[1], {})[o["e"]] = i
+        for j in o["after"]:
+            d.setdefault(j, False)
+        deps.append(d)
+
+    def hard(i, j):
+        if ops[j]["sem"] == "none":
+            return False
+        if ops[i]["e"] != ops[j]["e"] or ops[j]["sem"] or ops[i]["sem"]:
+            return True
+        return deps[i][j] and ops[i]["e"] != "P"
+    succ = [[] for _ in range(n)]
+    for i in range(n):
+        for j in deps[i]:
+            succ[j].append(i)
+    prio = [0.0] * n
+    for i in range(n - 1, -1, -1):
+        p = 0.0
+        for k in succ[i]:
+            p = max(p, prio[k] + ((ops[i]["lat"] + SYNC) if hard(k, i) else 0.0))
+        prio[i] = p + ops[i]["cost"]
+    tail = ("S1", "NQ", "S2", "R8", "CT", "EX", "EB", "O16", "OFF")
+    for i, o in enumerate(ops):
+        nm = o["w"][0][1] if o["w"] else ""
+        if nm[:-1] in tail or nm in ("CL", "UVL") or (o["e"] == "P" and o["r"][0][1][:2] in ("EX", "AB", "WI")):
+            prio[i] += OPT["boost"]
+        if nm == "OH" or (o["e"] == "P" and o["r"][0][1] == "SEL2"):
+            prio[i] += OPT["hb"]
+        if o["sem"] == "none":
+            prio[i] += 1e9
+    left = [len(d) for d in deps]
+    est = [0.0] * n
+    ready = {e: [] for e in "VSPGYR"}
+    for i in range(n):
+        if not left[i]:
+            ready[ops[i]["e"]].append(i)
+    free = {e: 0.0 for e in ready}
+    order = {e: [] for e in ready}
+    start = [0.0] * n
+    seq = []
+    for _ in range(n):
+        best = None
+        for e, r in ready.items():
+            if not r:
+                continue
+            t0 = max(free[e], min(est[i] for i in r))
+            c = max((i for i in r if est[i] <= t0 + OPT["look"]), key=lambda i: (prio[i], -i))
+            if est[c] > t0:
+                fill = [i for i in r if max(t0, est[i]) + ops[i]["cost"] <= est[c] + OPT["tol"] and est[i] < est[c]]
+                if fill:
+                    c = max(fill, key=lambda i: (prio[i], -i))
+            t1 = max(free[e], est[c])
+            if best is None or t1 < best[0]:
+                best = (t1, e, c)
+        t1, e, c = best
+        ready[e].remove(c); order[e].append(c); seq.append(c); start[c] = t1
+        free[e] = t1 + ops[c]["cost"]
+        for k in succ[c]:
+            est[k] = max(est[k], free[e] + ((ops[c]["lat"] + SYNC) if hard(k, c) else 0.0))
+            left[k] -= 1
+            if not left[k]:
+                ready[ops[k]["e"]].append(k)
+    count = {}
+    tick = [None] * n
+    for e in "VSPG":
+        for i in order[e]:
+            if not ops[i]["sem"]:
+                count["s" + e] = count.get("s" + e, 0) + 1
+                tick[i] = ("s" + e, count["s" + e])
+    for i, o in enumerate(ops):
+        if o["sem"] and o["sem"] != "none":
+            tick[i] = (o["sem"], 16 if o["sem"][0] == "d" else -1)
+            count[o["sem"]] = tick[i][1]
+    known = {e: {} for e in ready}
+    clock = [None] * n
+    waits = [None] * n
+    pos = {c: k for k, c in enumerate(seq)}
+    for i in seq:
+        e = ops[i]["e"]; kn = known[e]; w = {}
+        for j in sorted(deps[i], key=lambda j: -pos[j]):
+            if not hard(i, j):
+                continue
+            s, v = tick[j]
+            if kn.get(s, 0) >= abs(v):
+                continue
+            w[s] = max(w.get(s, 0), abs(v)) if v > 0 else -1
+            if ops[j]["e"] != "R":
+                for s2, v2 in clock[j].items():
+                    if kn.get(s2, 0) < v2:
+                        kn[s2] = v2
+            kn[s] = max(kn.get(s, 0), abs(v))
+        waits[i] = w
+        clock[i] = dict(kn)
+    total = max(start[i] + ops[i]["cost"] + ops[i]["lat"] for i in range(n))
+    return dict(ops=ops, seq=seq, tick=tick, waits=waits, count=count, total=total, start=start, deps=deps)
+
+
+PLAN = []
+
+
+def routes(T, topo):
+    n = len(T.cores); out = []
+
+    def share(eng, k):
+        p = 1
+        while 2 * p * k <= len(eng):
+            p *= 2
+        return [eng[i * p:(i + 1) * p] for i in range(k)]
+    for q, src in enumerate(T.cores):
+        dsts = [T.cores[(q + 1 + j) % n] for j in range(n - 1)]
+        direct = [j for j, d in enumerate(dsts) if topo.may_write(src, d)]
+        other = [j for j, d in enumerate(dsts) if j not in direct]
+        off = topo.engines(src, dsts[direct[0]]) if direct else []
+        mine = []
+        for j, e in zip(direct, share(off, max(1, len(direct)))):
+            mine.append((j, dsts[j], None, e[:4], None))
+        if other:
+            help_ = [c for c in topo.cores_of(src) if c != src and all(topo.may_write(c, dsts[j]) for j in other)]
+            help_.sort(key=lambda c: topo.die(c) != topo.die(src))
+            help_ = help_[:2]
+            on = [e for e in topo.engines(src, help_[0]) if e not in off]
+            per = {c: [j for k, j in enumerate(other) if help_[k % len(help_)] == c] for c in help_}
+            for k, (j, e) in enumerate(zip(other, share(on, len(other)))):
+                c = help_[k % len(help_)]
+                e2 = share(topo.engines(c, dsts[j]), len(per[c]))[per[c].index(j)]
+                mine.append((j, dsts[j], c, e, e2[:4]))
+        out.append(mine)
+    return out
+
+
+def write(T, topo, src, dst, engines, sem, a, b):
+    rid, pid = topo.addr(dst, src)
+    return RemoteDMATransfer(dst_ids=[DstId(rid=rid, pnc=pid)], dma_engine_mask=sum(1 << e for e in engines),
+                             remote_sem=T.sem[sem], src=a, dst=b)
+
+
+def rank_program(g, core, T, topo):
+    rank = T.rank_of(core)
+    rt = routes(T, topo)
+    if rank is None:
+        mine = [r for q in rt for r in q if r[2] == core]
+        if not mine:
+            return
+        sent = 0
+        for e in range(NT - 1):
+            g.wait_ge(T.sem["rel%d" % e], sum(len(r[3]) for r in mine))
+            land = T["LND%d" % e]
+            g.remote_dma_fused([write(T, topo, core, d, e2, "arr%d" % e, land[:, 16 * j:16 * j + 16], land[:, 16 * j:16 * j + 16])
+                                for j, d, c, e1, e2 in mine], local_sem=T.sem.sent)
+            sent += sum(len(r[4]) for r in mine)
+        g.wait_ge(T.sem.sent, sent)
+        return
+    if not PLAN:
+        PLAN.append(plan())
+    P = PLAN[0]
+    arrivals = sum(len(r[3] if r[2] is None else r[4]) for q in rt for r in q if r[1] == core)
+    queue = {"V": g.vector, "S": g.scalar, "P": g.tensor, "G": g, "Y": g.sync}
+    sent = 0
+    for i in P["seq"]:
+        o = P["ops"][i]
+        if o["e"] == "R":
+            continue
+        for s, v in P["waits"][i].items():
+            queue[o["e"]].wait_ge(T.sem[s], arrivals if v < 0 else v)
+        if o["sem"] == "none":
+            e = o["fn"][1]; snd, land = T["SND%d" % e], T["LND%d" % e]
+            g.remote_dma_fused([write(T, topo, core, d if c is None else c, e1, ("arr%d" if c is None else "rel%d") % e,
+                                      snd[:, 16 * j:16 * j + 16], land[:, 16 * j:16 * j + 16])
+                                for j, d, c, e1, e2 in rt[rank]], local_sem=T.sem.sent)
+            sent += sum(len(r[3]) for r in rt[rank])
+            continue
+        s, v = P["tick"][i]
+        o["fn"](g, T).then_inc(T.sem[s], 16 if o["sem"] else 1)
+    g.wait_ge(T.sem.sent, sent)
+    for s, v in P["count"].items():
+        if v > 0:
+            g.wait_ge(T.sem[s], v)

@@ -4,8 +4,8 @@ from concourse.bass import DstId, RemoteDMATransfer
 from concourse.mybir import AluOpType as ALU, ActivationFunctionType as AF
 
 L0, S, NT, HOPS, NEW, TRAVEL = 1152, 256, 3, 5, 32, 80
-OPT = dict(relu=True, nbs=(76, 76), chunk=2, arrive=6000.0, look=100.0, tol=70.0, boost=4000.0, hb=3000.0, nbby=3)
-COST = dict(gather=1.5, scatter=3.5, cyc=0.83, pe=0.42, sync=60.0, sfix=65.0)
+OPT = dict(relu=True, nbs=(78, 78), chunk=3, arrive=6000.0, look=100.0, tol=60.0, boost=8000.0, hb=3000.0, nbby=2)
+COST = dict(gather=1.5, scatter=3.5, cyc=0.83, pe=0.42, sync=130.0, sfix=65.0, pf=20.0, vf=20.0)
 F32, BF, F16, I32, U16 = "float32", "bfloat16", "float16", "int32", "uint16"
 BIGK = float(2 ** 23)
 LNB, LNH = math.log(2.2), math.log(1.9)
@@ -24,7 +24,7 @@ for n_, c_, d_ in [
     ("EL", 48, U16), ("EF", 48, F32), ("EH", 48, F16), ("CL", 16, U16), ("UVL", 32, U16), ("UVF", 32, F32),
     ("VUH", 32, F16), ("CK5", 16, F32), ("FX", 256, BF), ("THX", 256, F32), ("COL", 48, F32), ("COI", 64, I32),
     ("MAT", (17, 128), BF), ("M32", (4, 128), F32), ("SELT", (16, 128), BF), ("SEL", 144, BF), ("SEL2", 144, BF),
-    ("BC", 96, BF), ("WIDE", 240, BF), ("I17", 136, BF),
+    ("BC", 32, BF), ("I17", 136, BF), ("I17F", 136, F32),
     ("KC", (4, 136), BF), ("D0C", (2, 136), F32), ("DG", 32, F32), ("ZERO", 768, BF), ("IOF", 256, F32),
     ("NOH", 1280, BF), ("ZT", 1280, BF), ("THR", 256, BF), ("DL", 32, F32), ("PERM", 12, U16), ("XL", 80, U16),
     ("C1", 512, BF), ("C2", 512, BF), ("HALF", 512, BF), ("CW", 768, BF), ("C32", 256, BF), ("CN", 768, BF),
@@ -39,7 +39,7 @@ for n_, c_, d_ in [
 ]:
     sb(n_, c_, d_)
 for s_ in "AB":
-    for n_, c_, d_ in [("OFF", 128, U16), ("O16", 128, F16), ("EX", 128, F16), ("EB", 64, F16), ("DF", 2048, BF),
+    for n_, c_, d_ in [("OFF", 128, U16), ("O16", 128, F16), ("O32", 128, F32), ("EX", 128, F16), ("DF", 2048, BF),
                        ("WG", 2048, BF), ("AB", 2048, BF), ("S1", 136, F32), ("NQ", 136, BF), ("S2", 136, F32),
                        ("D0", 136, F32), ("R8", 8, F32), ("CT", 8, F32), ("E0", 256, BF)]:
         sb(n_ + s_, c_, d_)
@@ -133,7 +133,7 @@ def build(t_ops):
         f = 0.5 if two(out) and all(two(i) for i in ins) else 1.0
         if slow:
             f = 1.0 if any(psum(i) for i in ins) else 2.0
-        return max(64, n * f) * CYC + 10
+        return max(64, n * f) * CYC + 10 + COST["vf"]
 
     def cp(out, in_):
         op("V", lambda g, T: g.vector.tensor_copy(res(T, out), res(T, in_)), [in_], [out], vcost(out, [in_]))
@@ -164,7 +164,7 @@ def build(t_ops):
            [in_, bias, scale], [out] + ([acc] if acc else []), c)
 
     def mm(out, lhsT, rhs, start, stop):
-        c = max(64, cols(rhs)[1]) * PECYC * (1 if two(rhs) else 4)
+        c = max(64, cols(rhs)[1]) * PECYC * (1 if two(rhs) else 4) + COST["pf"]
         op("P", lambda g, T: g.tensor.matmul(res(T, out), res(T, lhsT), res(T, rhs), start, stop), [lhsT, rhs], [out], c, 60)
 
     def group(items):
@@ -205,8 +205,7 @@ def build(t_ops):
 
     ID, NID, BO, NBO, LA, LT, I75, I25, I875, I125, I50, I256, IB, NIB, I2K, NI2K, DGM = [A("MAT", i) for i in range(17)]
     I32M, NI32M, ONE32, THB = [A("M32", i) for i in range(4)]
-    BC1, BC128, NBC64, BMR = C("BC", 0, 8), C("BC", 8, 16), C("BC", 16, 24), C("BC", 32, 96)
-    L8 = C("PERM", 6, 10)
+    BC1, BC128, NBC64 = C("BC", 0, 8), C("BC", 8, 16), C("BC", 16, 24)
     relu = OPT["relu"]
     prev = {"NB": []}
 
@@ -239,15 +238,10 @@ def build(t_ops):
     cp(A("XL"), C("G2", 0, 80))
     cp(C("COL", 32, 40), C("G2", 0, 8))
     ts(BC1, C("COL", 32, 40), cG, ALU.is_equal)
-    ms(A("WIDE"), 0.0); cp(C("WIDE", 112, 128), C("DG", 0, 16))
-    iota(C("G2", 128, 132), [[2, 4]], 0, 0)
-    ts(C("COL", 3), cI, 8.0, ALU.is_ge)
-    ts(L8, C("G2", 128, 132), C("COL", 3), ALU.add)
-    iota(C("THX", 0, 64), [[0, 8], [1, 8]], 0, 0)
-    ts(BMR, C("THX", 0, 64), cG, ALU.is_equal)
     ts(BC128, BC1, 128.0, ALU.mult); ts(NBC64, BC1, -64.0, ALU.mult)
     aff(A("I17"), C("ZERO", 0, 136), [[16, 8], [1, 17]], ALU.not_equal, 1.0, -1, -1)
     ms(C("I17", 0, 136, 17), 0.0)
+    gcopy(A("I17F"), A("I17"))
     iota(A("KC", 1), [[0, 8], [1, 17]], 0, 0)
     iota(C("IOF", 0, 136), [[1, 8], [0, 17]], 0, 0)
     ts(A("KC", 0), C("IOF", 0, 136), float(2 ** 19), ALU.mult)
@@ -358,13 +352,17 @@ def build(t_ops):
             lst = C("EL", 16 * t + lo, 16 * t + lo + 8)
         else:
             lst = C("UVL" if h == HOPS else "CL", lo, lo + 8)
-        ids = A("IDI") if t == 0 and h == 0 else A("IDF")
-        cp(A("O16" + n), IND(ids, lst))
+        first = t == 0 and h == 0
+        ids = A("IDI") if first else A("IDF")
+        cp(A("O16" + n if first else "OFF" + n), IND(ids, lst))
         if 2 * h + s >= OPT["nbby"] and prev["NB"]:
             after(prev["NB"].pop(0))
         if t == 0 and 2 * h + s == 2:
             after(prev["exp"])
-        cp(A("OFF" + n), A("O16" + n))
+        if first:
+            cp(A("OFF" + n), A("O16" + n))
+        else:
+            act(A("O32" + n), IND(ids, lst), AF.Copy)
         nb = OPT["nbs"][s]
         parts = [(b, min(nb, b + 32)) for b in range(0, nb, 32)]
         for b, e in parts:
@@ -384,7 +382,7 @@ def build(t_ops):
             else:
                 act(ab, d, AF.Abs, scale=0.5)
         key, idt = C(K, 0, 136), C(K, 136, 272)
-        items = [(idt, ID, A("KC", 3)), (idt, A("O16" + n), A("I17"))]
+        items = [(idt, ID, A("KC", 3)), (idt, A("O16" + n), A("I17")) if first else (idt, A("O32" + n), A("I17F"))]
         if h == 0:
             tt(C("E0" + n, 0, 128), IND(A("W"), lst), C("X", 256 * t + 128 * s, 256 * t + 128 * s + 128), ALU.subtract)
             act(C("E0" + n, 128, 256), C("E0" + n, 0, 128), AF.Abs, scale=0.5)
@@ -412,9 +410,9 @@ def build(t_ops):
         last = C("S2" + n, 16, 136, 17)
         ts(A("R8" + n), last, 1.5 * 2 ** 35, ALU.add, 1.5 * 2 ** 35, ALU.subtract)
         tt(A("CT" + n), last, A("R8" + n), ALU.subtract)
-        tt(A("EB" + n), IND(A("CT" + n), L8), BMR, ALU.mult)
         lp = C(K, 272, 280)
-        group([(lp, C("WIDE", 112 - 16 * k, 240 - 16 * k), C("EB" + n, 8 * k, 8 * k + 8)) for k in range(8)])
+        tt(A("EX" + n), IND(A("CT" + n), C("XL", 0, 8)), DGM, ALU.mult)
+        mm(lp, A("EX" + n), BC1, True, True)
         if h < HOPS - 1:
             cp(C("CL", lo, lo + 8), lp)
         else:
@@ -637,10 +635,10 @@ def plan():
         for k in succ[i]:
             p = max(p, prio[k] + ((ops[i]["lat"] + SYNC) if hard(k, i) else 0.0))
         prio[i] = p + ops[i]["cost"]
-    tail = ("S1", "NQ", "S2", "R8", "CT", "EX", "EB", "O16", "OFF")
+    tail = ("S1", "NQ", "S2", "R8", "CT", "EX", "O16", "OFF")
     for i, o in enumerate(ops):
         nm = o["w"][0][1] if o["w"] else ""
-        if nm[:-1] in tail or nm in ("CL", "UVL") or (o["e"] == "P" and o["r"][0][1][:2] in ("EX", "AB", "WI")):
+        if nm[:-1] in tail or nm in ("CL", "UVL") or (o["e"] == "P" and o["r"][0][1][:2] in ("EX", "AB")):
             prio[i] += OPT["boost"]
         if nm == "OH" or (o["e"] == "P" and o["r"][0][1] == "SEL2"):
             prio[i] += OPT["hb"]

import math
import numpy as np
from concourse.bass import DstId, RemoteDMATransfer
from concourse.mybir import AluOpType as ALU, ActivationFunctionType as AF

L0, S, NT, HOPS, NEW, TRAVEL = 1152, 256, 3, 5, 32, 80
OPT = dict(relu=True, nbs=(78, 78), chunk=3, arrive=6000.0, look=100.0, tol=60.0, boost=8000.0, hb=3000.0, nbby=2)
COST = dict(gather=1.5, scatter=3.5, cyc=0.83, pe=0.42, sync=130.0, sfix=65.0, pf=20.0, vf=20.0)
F32, BF, F16, I32, U16 = "float32", "bfloat16", "float16", "int32", "uint16"
BIGK = float(2 ** 23)
LNB, LNH = math.log(2.2), math.log(1.9)
MAGIC = 1.5 * 2 ** 23

SCRATCH = {}


def sb(name, cols, dt):
    SCRATCH[name] = ("sbuf", [128] + (list(cols) if isinstance(cols, tuple) else [cols]), dt)


for n_, c_, d_ in [
    ("W", 2048, F32), ("WB", 1248, BF), ("NBI", 1152, I32), ("IDI", 1152, I32), ("IDF", 1792, F32), ("NB", 1792, F32),
    ("X", 768, BF), ("ENT", 48, I32), ("THI", 8, I32), ("XR0", 4096, BF), ("XR1", 4096, BF),
    ("EL", 48, U16), ("EF", 48, F32), ("EH", 48, F16), ("CL", 16, U16), ("UVL", 32, U16), ("UVF", 32, F32),
    ("VUH", 32, F16), ("CK5", 16, F32), ("FX", 256, BF), ("THX", 256, F32), ("COL", 48, F32), ("COI", 64, I32),
    ("MAT", (17, 128), BF), ("M32", (4, 128), F32), ("SELT", (16, 128), BF), ("SEL", 144, BF), ("SEL2", 144, BF),
    ("BC", 32, BF), ("I17", 136, BF), ("I17F", 136, F32),
    ("KC", (4, 136), BF), ("D0C", (2, 136), F32), ("DG", 32, F32), ("ZERO", 768, BF), ("IOF", 256, F32),
    ("NOH", 1280, BF), ("ZT", 1280, BF), ("THR", 256, BF), ("DL", 32, F32), ("PERM", 12, U16), ("XL", 80, U16),
    ("C1", 512, BF), ("C2", 512, BF), ("HALF", 512, BF), ("CW", 768, BF), ("C32", 256, BF), ("CN", 768, BF),
    ("PKS0", 264, F32), ("PKS1", 264, F32), ("PKO", 160, F32), ("SND0", 80, F32), ("SND1", 80, F32),
    ("LND0", 80, F32), ("LND1", 80, F32), ("NW", 80, F32), ("NWI", 240, I32), ("NWH", 80, F16),
    ("THS", 512, BF), ("ZS", 512, BF), ("OH", (4, 128), BF), ("OL", (4, 8, 80), BF), ("FS", 640, F32), ("LOI", 32, I32),
    ("LOL", 32, U16), ("BAD", 512, BF), ("WANT", 256, BF), ("P1C", 272, BF), ("PFAR", 256, BF), ("JUNK", 1792, BF),
    ("RS", 8, F32), ("RL", 8, U16), ("OFT", 64, F32), ("OFL", 32, U16), ("TGS", 528, F32), ("TP", 512, F16),
    ("TT", 520, F32), ("AG", 512, BF), ("EA", 512, BF), ("HH", 256, BF), ("MT", 512, BF), ("SG", 512, BF),
    ("Z1", 512, F32), ("Z2", 512, F32), ("M1", 512, F32), ("M2", 512, F32), ("WUV", 512, BF), ("WR", 776, F32),
    ("G1", 128, F32), ("G2", 136, F32),
]:
    sb(n_, c_, d_)
for s_ in "AB":
    for n_, c_, d_ in [("OFF", 128, U16), ("O16", 128, F16), ("O32", 128, F32), ("EX", 128, F16), ("DF", 2048, BF),
                       ("WG", 2048, BF), ("AB", 2048, BF), ("S1", 136, F32), ("NQ", 136, BF), ("S2", 136, F32),
                       ("D0", 136, F32), ("R8", 8, F32), ("CT", 8, F32), ("E0", 256, BF)]:
        sb(n_ + s_, c_, d_)
for n_ in ("P0", "P1", "P2", "P3", "P4", "P5", "P6"):
    SCRATCH[n_] = ("psum", [128, 512], F32)
SCRATCH["PB"] = ("psum", [128, 1024], BF)

SEMAPHORES = ["sV", "sS", "sP", "sG", "arr0", "arr1", "rel0", "rel1", "sent"] + ["d%d" % i for i in range(12)]

ALL = slice(None)


def A(name, *idx):
    return ("ap", name, idx)


def C(name, a, b=None, step=None):
    return A(name, slice(a, a + 1) if b is None else slice(a, b, step))


def IND(win, off):
    return ("ind", win, off)


def is_ap(v):
    return isinstance(v, tuple) and len(v) == 3 and v[0] in ("ap", "ind", "io")


def res(T, v):
    if not is_ap(v):
        return v
    if v[0] == "ind":
        return res(T, v[1]).indirect(res(T, v[2]))
    if v[0] == "io":
        return T[v[1]][v[2]]
    return T[v[1]][(ALL,) + v[2]]


MASKS = {}


def cols(v):
    key = repr(v)
    if key not in MASKS:
        shape = SCRATCH[v[1]][1][1:]
        c = np.arange(int(np.prod(shape))).reshape(shape)[v[2]].ravel()
        m = 0
        for i in c.tolist():
            m |= 1 << i
        MASKS[key] = (m, len(c))
    return MASKS[key]


def two(v):
    return SCRATCH[v[1]][2] in (BF, F16, U16)


def psum(v):
    return SCRATCH[v[1]][0] == "psum"


def build(t_ops):
    GATHER, SCATTER, CYC, PECYC = COST["gather"], COST["scatter"], COST["cyc"], COST["pe"]

    def op(e, fn, reads, writes, cost, lat=0.0, sem=None):
        r, w = [], []
        for v in reads:
            if is_ap(v) and v[0] == "ind":
                r += [v[1], v[2]]
            elif is_ap(v) and v[0] == "ap":
                r.append(v)
        for v in writes:
            if v[0] == "ind":
                w.append(v[1]); r.append(v[2])
            elif v[0] == "ap":
                w.append(v)
        t_ops.append(dict(e=e, fn=fn, r=r, w=w, cost=cost, lat=lat, sem=sem, after=[]))

    def here():
        return len(t_ops) - 1

    def after(j):
        t_ops[-1]["after"].append(j)

    def vcost(out, ins, slow=False):
        n = cols(ins[0])[1] if out[0] == "ind" else cols(out)[1]
        if out[0] == "ind":
            return 50 + n * SCATTER * CYC
        if ins[0][0] == "ind":
            return 50 + n * GATHER * CYC
        f = 0.5 if two(out) and all(two(i) for i in ins) else 1.0
        if slow:
            f = 1.0 if any(psum(i) for i in ins) else 2.0
        return max(64, n * f) * CYC + 10 + COST["vf"]

    def cp(out, in_):
        op("V", lambda g, T: g.vector.tensor_copy(res(T, out), res(T, in_)), [in_], [out], vcost(out, [in_]))

    def tt(out, a, b, o):
        op("V", lambda g, T: g.vector.tensor_tensor(res(T, out), res(T, a), res(T, b), o), [a, b], [out],
           vcost(out, [a, b], True))

    def ts(out, a, s1, o0, s2=None, o1=None):
        def fn(g, T):
            if o1 is None:
                return g.vector.tensor_scalar(res(T, out), res(T, a), res(T, s1), None, o0)
            return g.vector.tensor_scalar(res(T, out), res(T, a), res(T, s1), res(T, s2), o0, o1)
        op("V", fn, [a, s1, s2], [out], vcost(out, [a]))

    def scan(out, d0, d1, o0, o1):
        op("V", lambda g, T: g.vector.tensor_tensor_scan(res(T, out), res(T, d0), res(T, d1), 0.0, o0, o1), [d0, d1], [out],
           vcost(out, [d0, d1]))

    def ms(out, val):
        op("V", lambda g, T: g.vector.memset(res(T, out), val), [], [out], vcost(out, [out]))

    def act(out, in_, f, bias=0.0, scale=1.0, acc=None, extra=0.0):
        n = cols(out)[1]
        c = COST["sfix"] + extra + n * CYC * (GATHER if in_[0] == "ind" else 1.0)
        op("S", lambda g, T: g.scalar.activation(res(T, out), res(T, in_), f, bias=res(T, bias), scale=res(T, scale),
                                                 accum_out=res(T, acc)),
           [in_, bias, scale], [out] + ([acc] if acc else []), c)

    def mm(out, lhsT, rhs, start, stop):
        c = max(64, cols(rhs)[1]) * PECYC * (1 if two(rhs) else 4) + COST["pf"]
        op("P", lambda g, T: g.tensor.matmul(res(T, out), res(T, lhsT), res(T, rhs), start, stop), [lhsT, rhs], [out], c, 60)

    def group(items):
        for i, (o, l, r) in enumerate(items):
            mm(o, l, r, i == 0, i == len(items) - 1)

    def ptr(out, in_, ident):
        op("P", lambda g, T: g.tensor.transpose(res(T, out), res(T, in_), res(T, ident)), [in_, ident], [out], 128 * PECYC, 60)

    def iota(out, pat, base, cm):
        flag = SCRATCH[out[1]][2] != I32

        def fn(g, T):
            if flag:
                return g.iota(res(T, out), pat, base, cm, allow_small_or_imprecise_dtypes=True)
            return g.iota(res(T, out), pat, base, cm)
        op("G", fn, [], [out], 130 + 2 * CYC * cols(out)[1])

    def aff(out, in_, pat, cmp_, fill, base, cm):
        op("G", lambda g, T: g.affine_select(res(T, out), res(T, in_), pat, cmp_, fill, base, cm), [in_], [out],
           170 + 2 * CYC * cols(out)[1])

    def gcopy(out, in_):
        aff(out, in_, [[0, cols(out)[1]]], ALU.is_ge, 0.0, 0, 0)

    def gfill(out, val):
        n = cols(out)[1]
        aff(out, C("ZERO", 0, n), [[0, n]], ALU.is_gt, val, 0, 0)

    nd = [0]

    def dma(q, out, in_, lat):
        sem = "d%d" % nd[0]; nd[0] += 1
        if q == "Y":
            op("Y", lambda g, T: g.sync.dma_start(res(T, out), res(T, in_)), [in_], [out], 60, lat, sem)
        else:
            op("S", lambda g, T: g.scalar.dma_start(res(T, out), res(T, in_)), [in_], [out], 60, lat, sem)

    ID, NID, BO, NBO, LA, LT, I75, I25, I875, I125, I50, I256, IB, NIB, I2K, NI2K, DGM = [A("MAT", i) for i in range(17)]
    I32M, NI32M, ONE32, THB = [A("M32", i) for i in range(4)]
    BC1, BC128, NBC64 = C("BC", 0, 8), C("BC", 8, 16), C("BC", 16, 24)
    relu = OPT["relu"]
    prev = {"NB": []}

    def sel(a, name="SEL"):
        return C(name, 15 - a, 143 - a)

    dma("Y", C("X", 0, 256), ("io", "x", (ALL, slice(0, 256))), 2000)
    dma("S", A("ENT"), ("io", "ent", (ALL,)), 2000)
    dma("Y", A("NBI"), ("io", "nb", (ALL,)), 3200)
    dma("S", C("WB", 0, L0), ("io", "w", (ALL,)), 2600)
    dma("Y", C("X", 256, 768), ("io", "x", (ALL, slice(256, 768))), 3600)
    dma("Y", C("THI", 0), ("io", "th", (ALL,)), 2500)

    ms(A("ZERO"), 0.0)
    ms(C("W", L0, 2047), 0.0); ms(C("W", 2047), 512.0)
    Z128 = C("ZERO", 0, 128)

    def diag(out, val):
        aff(out, Z128, [[-1, 128]], ALU.not_equal, val, 0, 1)
    diag(ID, 1.0); diag(NID, -1.0); diag(I32M, 1.0)
    iota(C("COI", 0), [[0, 1]], 0, 1)
    ts(C("COI", 1), C("COI", 0), 15, ALU.bitwise_and)
    ts(C("COI", 2), C("COI", 0), 4, ALU.logical_shift_right)
    cI, cG = C("COL", 1), C("COL", 2)
    cp(C("COL", 1, 3), C("COI", 1, 3))
    iota(C("G1", 0, 128), [[0, 8], [1, 16]], 0, 0)
    ts(DGM, C("G1", 0, 128), cI, ALU.is_equal)
    ts(C("DG", 0, 16), C("G1", 0, 16), cI, ALU.is_equal)
    iota(C("G2", 0, 80), [[1, 80]], 0, 0)
    cp(A("XL"), C("G2", 0, 80))
    cp(C("COL", 32, 40), C("G2", 0, 8))
    ts(BC1, C("COL", 32, 40), cG, ALU.is_equal)
    ts(BC128, BC1, 128.0, ALU.mult); ts(NBC64, BC1, -64.0, ALU.mult)
    aff(A("I17"), C("ZERO", 0, 136), [[16, 8], [1, 17]], ALU.not_equal, 1.0, -1, -1)
    ms(C("I17", 0, 136, 17), 0.0)
    gcopy(A("I17F"), A("I17"))
    iota(A("KC", 1), [[0, 8], [1, 17]], 0, 0)
    iota(C("IOF", 0, 136), [[1, 8], [0, 17]], 0, 0)
    ts(A("KC", 0), C("IOF", 0, 136), float(2 ** 19), ALU.mult)
    cp(A("KC", 2), A("KC", 0)); ms(A("KC", 2, slice(0, 136, 17)), BIGK)
    iota(C("FS", 0, 136), [[32, 8], [-1, 17]], 16, 0)
    ts(A("KC", 3), C("FS", 0, 136), 4096.0, ALU.mult)
    ms(A("D0C"), 0.0); ms(A("D0C", 0, slice(0, 136, 17)), BIGK)
    ts(A("D0C", 1, slice(0, 136, 17)), C("IOF", 0, 136, 17), float(2 ** 19), ALU.mult, 64.0 * 4090, ALU.add)
    ms(A("D0A"), 0.0); ms(A("D0B"), 0.0)
    if relu:
        for s in range(2):
            ms(C("DF" + "AB"[s], 0, 16 * OPT["nbs"][s]), 0.0)

    cp(A("EL"), A("ENT")); cp(A("EF"), A("ENT"))
    for i in range(16):
        cp(C("XR0", i, 2048, 16), C("X", 0, 128))
    for i in range(16):
        if i < 8:
            act(C("XR0", 2048 + i, 4096, 16), C("X", 128, 256), AF.Copy)
        else:
            cp(C("XR0", 2048 + i, 4096, 16), C("X", 128, 256))
    act(C("W", 0, L0), C("WB", 0, L0), AF.Copy)
    ts(A("IDI"), A("NBI"), 2047, ALU.bitwise_and)
    gcopy(C("IDF", 0, L0), A("IDI"))
    gfill(C("IDF", L0, 1792), 2047.0)

    def late_setup():
        gcopy(C("NB", 0, L0), A("NBI")); gfill(C("NB", L0, 1792), 32767.0)
        for m, v in [(I75, .75), (I25, .25), (I875, .875), (I125, .125), (I50, .5), (I256, 1 / 256), (IB, 32768.0),
                     (NIB, -32768.0), (I2K, 2048.0), (NI2K, -2048.0), (NI32M, -1.0)]:
            diag(m, v)
        gfill(ONE32, 1.0)
        aff(BO, ONE32, [[-16, 8], [0, 16]], ALU.is_ge, 0.0, 0, 1)
        aff(BO, BO, [[16, 8], [0, 16]], ALU.is_ge, 0.0, 15, -1)
        ts(NBO, BO, -1.0, ALU.mult)
        gfill(A("SEL"), 0.0); gfill(A("SEL2"), 0.0)
        ts(C("SEL", 15, 143, 16), BC1, 64.0, ALU.mult)
        ts(C("SEL2", 15, 143, 16), BC1, 2048.0, ALU.mult)
        for a in range(16):
            ts(A("SELT", a), BO, C("DG", a), ALU.mult)
        ts(C("COL", 5), cI, 12.0, ALU.is_lt)
        ts(C("COL", 6), cI, -LNB, ALU.mult, 11 * LNB - 80, ALU.add)
        act(C("COL", 7), C("COL", 6), AF.Exp, bias=192 * LNB, extra=1300)
        prev["exp"] = here()
        aff(LA, BO, [[-1, 128]], ALU.not_equal, -1.0, 0, 1)
        ts(LA, LA, C("COL", 5), ALU.mult)
        ts(LT, LA, C("COL", 7), ALU.mult)
        ts(C("COL", 8), cI, 12.0, ALU.is_ge)
        ts(C("COL", 9), cI, 2.0, ALU.is_ge, C("COL", 5), ALU.mult)
        ts(C("COL", 9), C("COL", 9), 32767.0, ALU.mult)
        ts(C("COL", 10), cG, 80.0, ALU.mult, -0.46875, ALU.add)
        ts(C("COL", 11), C("COL", 5), -2048.0, ALU.mult, -1024.0, ALU.add)
        ts(C("C1", 0, 256), C("ZERO", 0, 256), C("COL", 11), ALU.add)
        gfill(C("C1", 256, 512), -1024.0); gfill(A("C2"), -31744.0); gfill(A("HALF"), -0.5)
        gfill(C("CW", 0, 256), -0.375); gfill(C("CW", 256, 512), -0.4375); gfill(C("CW", 512, 768), -0.25)
        gfill(A("C32"), 32.0)
        for t in range(NT):
            gfill(C("CN", 256 * t, 256 * t + 256), -896.0 + 32 * t)
        gfill(C("P1C", 0, 16), 0.0)
        gfill(C("TT", 256, 264), 32767 - 1023.5); gfill(C("TGS", 256, 264), 32767.0); gfill(C("TGS", 520, 528), 32767.0)
        gfill(C("WR", 768, 776), MAGIC)
        gfill(C("PKS0", 256, 264), 0.0); gfill(C("PKS1", 256, 264), 0.0)
        iota(A("IOF"), [[1, 256]], 0, 0)
        act(A("THR"), A("IOF"), AF.Exp, bias=80 + math.log(2.5), scale=-LNH)
        iota(C("COL", 14, 16), [[128, 2]], 0, 1)
        act(C("COL", 12, 14), C("COL", 14, 16), AF.Exp, bias=80.0, scale=-LNH)
        ts(C("DG", 16, 32), C("DG", 0, 16), -1.0, ALU.mult, 1.0, ALU.add)
        ts(C("NOH", 0, 16), C("DG", 16, 32), float(2 ** 62), ALU.mult, float(2 ** 62), ALU.mult)
        n = 16
        while n < 1280:
            m = min(n, 1280 - n)
            gcopy(C("NOH", n, n + m), C("NOH", 0, m)); n += m
        for i in range(16):
            gcopy(C("ZT", i, 256, 16), C("DG", 0, 16))
        for k in range(1, 5):
            ts(C("ZT", 256 * k, 256 * k + 256), C("ZT", 0, 256), float(k + 1), ALU.mult)
        iota(C("G2", 96, 128), [[16, 32]], 1280, 0)
        ts(A("DL"), C("G2", 96, 128), cI, ALU.add)
        ts(C("COL", 40), cI, 5.0, ALU.mult, 0.5, ALU.add)
        ts(C("COL", 16, 21), C("COL", 32, 37), C("COL", 40), ALU.add)
        ts(C("COL", 41), cI, 0.5, ALU.add)
        ts(C("COL", 22, 24), C("COL", 32, 34), 16.0, ALU.mult, C("COL", 41), ALU.add)
        ts(C("COL", 24, 30), C("COL", 32, 38), 16.0, ALU.mult, cI, ALU.add)
        ts(C("COI", 8, 14), C("COL", 24, 30), -2.0, ALU.add, 0.2, ALU.mult)
        ts(C("COL", 42, 48), C("COI", 8, 14), -79.0, ALU.mult)
        ts(C("COL", 24, 30), C("COL", 24, 30), 16.0, ALU.mult)
        tt(C("COL", 42, 48), C("COL", 42, 48), C("COL", 24, 30), ALU.add)
        cp(C("PERM", 0, 6), C("COL", 42, 48))
        cp(C("COL", 30), C("THI", 0))
        ts(THB, BO, C("COL", 30), ALU.mult, 4.0, ALU.mult)
        mm(C("P6", 0, 128), ONE32, THB, True, True)
        iota(C("THX", 128, 256), [[1, 8], [0, 16]], 0, 0)
        ts(C("THX", 128, 256), C("THX", 128, 256), float(2 ** 19), ALU.mult)
        tt(C("THX", 0, 128), C("THX", 128, 256), C("P6", 0, 128), ALU.add)
        cp(A("EH"), A("ENT"))
        group([(A("P6"), I256, C("X", 0, 512))] + [(C("P6", a, 512, 16), A("SELT", a), C("EH", 0, 32)) for a in range(16)])
        act(C("PKS0", 0, 256), C("P6", 0, 256), AF.Identity, bias=float(2 ** 19), scale=256.0)
        act(C("PKS1", 0, 176), C("P6", 256, 432), AF.Identity, bias=float(2 ** 19), scale=256.0)
        act(C("PKO", 0, 80), C("P6", 432, 512), AF.Identity, scale=256.0)
        group([(C("P6", 0, 80), I256, C("X", 688, 768))] +
              [(C("P6", a, 80, 16), A("SELT", a), C("EH", 43, 48)) for a in range(16)])
        act(C("PKO", 80, 160), C("P6", 0, 80), AF.Identity, scale=256.0)

    def near(t, h, s):
        n = "AB"[s]; K = "P%d" % s; banks = ("P2", "P3") if s == 0 else ("P4", "P5")
        XR = "XR%d" % (t % 2); x0 = 2048 * s; lo = 8 * s
        if h == 0:
            lst = C("EL", 16 * t + lo, 16 * t + lo + 8)
        else:
            lst = C("UVL" if h == HOPS else "CL", lo, lo + 8)
        first = t == 0 and h == 0
        ids = A("IDI") if first else A("IDF")
        cp(A("O16" + n if first else "OFF" + n), IND(ids, lst))
        if 2 * h + s >= OPT["nbby"] and prev["NB"]:
            after(prev["NB"].pop(0))
        if t == 0 and 2 * h + s == 2:
            after(prev["exp"])
        if first:
            cp(A("OFF" + n), A("O16" + n))
        else:
            act(A("O32" + n), IND(ids, lst), AF.Copy)
        nb = OPT["nbs"][s]
        parts = [(b, min(nb, b + 32)) for b in range(0, nb, 32)]
        for b, e in parts:
            act(C("WG" + n, 16 * b, 16 * e), IND(A("W"), C("OFF" + n, b, e)), AF.Copy)
            if b == 0 and "S" in prev:
                after(prev["S"])
        k = OPT["chunk"]
        cut = [nb + 2 * (((128 - nb) // 2 * i) // k) for i in range(k + 1)]
        for b, e in zip(cut, cut[1:]):
            d, ab = C("DF" + n, 16 * b, 16 * e), C("AB" + n, 16 * b, 16 * e)
            tt(d, IND(A("W"), C("OFF" + n, b, e)), C(XR, x0 + 16 * b, x0 + 16 * e), ALU.subtract)
            if b == nb and "V" in prev:
                after(prev["V"])
            prev["V"] = here()
            if relu:
                ts(ab, d, 0.0, ALU.max)
            else:
                act(ab, d, AF.Abs, scale=0.5)
        key, idt = C(K, 0, 136), C(K, 136, 272)
        items = [(idt, ID, A("KC", 3)), (idt, A("O16" + n), A("I17")) if first else (idt, A("O32" + n), A("I17F"))]
        if h == 0:
            tt(C("E0" + n, 0, 128), IND(A("W"), lst), C("X", 256 * t + 128 * s, 256 * t + 128 * s + 128), ALU.subtract)
            act(C("E0" + n, 128, 256), C("E0" + n, 0, 128), AF.Abs, scale=0.5)
            tt(A("EX" + n), IND(C("EF", 16 * t + lo, 16 * t + lo + 8), C("XL", 0, 8)), DGM, ALU.mult)
            items.append((C(K, 136, 272, 17), A("EX" + n), BC1))
        elif h < HOPS:
            items.append((C(K, 136, 272, 17), I32M, A("CT" + n)))
        group(items)
        for k, (b, e) in enumerate(parts):
            o = C(banks[k % 2], 0, 16 * (e - b))
            group([(o, NID, C(XR, x0 + 16 * b, x0 + 16 * e)), (o, ID, C("WG" + n, 16 * b, 16 * e))])
            act(C("AB" + n, 16 * b, 16 * e), o, AF.Abs, scale=0.5)
            prev["S"] = here()
        items = [(key, ID, A("KC", 0 if h == 0 else 2)), (key, ID, A("KC", 1))]
        if h == 0:
            items.append((C(K, 0, 136, 17), C("E0" + n, 128, 256), BC128))
        if relu:
            items += [(C(K, 1 + i, 136, 17), C("DF" + n, i, 2048, 16), NBC64) for i in range(16)]
        items += [(C(K, 1 + i, 136, 17), C("AB" + n, i, 2048, 16), BC128) for i in range(16)]
        group(items)
        d0 = A("D0C", 0) if h == 0 else A("D0C", 1) if h == HOPS else A("D0" + n)
        scan(A("S1" + n), d0, key, ALU.max, ALU.min)
        tt(A("NQ" + n), A("S1" + n), key, ALU.not_equal)
        scan(A("S2" + n), A("NQ" + n), idt, ALU.mult, ALU.max)
        last = C("S2" + n, 16, 136, 17)
        ts(A("R8" + n), last, 1.5 * 2 ** 35, ALU.add, 1.5 * 2 ** 35, ALU.subtract)
        tt(A("CT" + n), last, A("R8" + n), ALU.subtract)
        lp = C(K, 272, 280)
        tt(A("EX" + n), IND(A("CT" + n), C("XL", 0, 8)), DGM, ALU.mult)
        mm(lp, A("EX" + n), BC1, True, True)
        if h < HOPS - 1:
            cp(C("CL", lo, lo + 8), lp)
        else:
            q = h - HOPS + 1
            cp(C("UVL", 16 * q + lo, 16 * q + lo + 8), lp)
            cp(C("UVF", 16 * q + lo, 16 * q + lo + 8), lp)
            cp(C("VUH", 16 - 16 * q + lo, 24 - 16 * q + lo), lp)
        if h < HOPS:
            o = C("D0" + n, 0, 136, 17) if h < HOPS - 1 else C("CK5", lo, lo + 8)
            ts(o, C("S1" + n, 16, 136, 17), 1.5 * 2 ** 29, ALU.add, 1.5 * 2 ** 29, ALU.subtract)

    def item(t, q):
        lst = C("UVL", 16 * q, 16 * q + 16); a, b = 256 * q, 256 * q + 256
        act(C("ZS", a, b), IND(A("ZT"), lst), AF.Copy)
        tt(C("THS", a, b), IND(A("NOH"), lst), A("THR"), ALU.max)
        ts(C("LOI", 16 * q, 16 * q + 16), C("UVF", 16 * q, 16 * q + 16), 1 / 16, ALU.mult, C("COL", 10), ALU.add)
        cp(C("LOL", 16 * q, 16 * q + 16), C("LOI", 16 * q, 16 * q + 16))
        for h in range(2):
            ptr(C("PB", a + 128 * h, a + 128 * h + 128), C("ZS", a + 128 * h, a + 128 * h + 128), ID)
        for h in range(2):
            mm(C("P6", 128 * h, 128 * h + 128), C("THS", a + 128 * h, a + 128 * h + 128), ID, True, True)
        act(A("OH", slice(2 * q, 2 * q + 2)), C("P6", 0, 256), AF.Relu, bias=1.0, scale=-2.0 ** -124)
        for h in range(2):
            for k in range(5):
                ts(A("OL", 2 * q + h, ALL, slice(16 * k, 16 * k + 16)), C("PB", a + 128 * h, a + 128 * h + 128),
                   float(k + 1), ALU.is_equal, C("COL", 12 + h), ALU.mult)
        c = 264 * q
        act(C("TT", c, c + 256), IND(A("NB"), lst), AF.Identity, bias=-1023.5)
        ts(C("AG", a, b), C("TT", c, c + 256), 1.5 * 2 ** 34, ALU.add, 1.5 * 2 ** 34, ALU.subtract)
        act(C("EA", a, b), C("AG", a, b), AF.Exp, bias=C("COL", 6), scale=12 * LNB / 2048)
        if q == 0:
            act(A("HH"), C("AG", 0, 256), AF.Relu, bias=-245760.0, scale=16.0)
        act(C("WUV", a, b), IND(A("W"), lst), AF.Copy)
        x = C("X", 256 * t, 256 * t + 256)
        o = C("P4" if q else "P6", 256, 512)
        group([(o, ID, C("CW", a, b)), (o, I125 if q else I25, x), (o, I875 if q else I75, C("WUV", a, b))])
        act(C("WR", a, b), o, AF.Identity, bias=MAGIC)
        k = "P5" if q else "P6"
        group([(C(k, i, 256, 16), A("SELT", i), C("VUH", 16 - 16 * q, 32 - 16 * q)) for i in range(16)])
        act(C("TGS", 264 - c, 520 - c), C(k, 0, 256), AF.Copy)
        if q == 0:
            group([(o, ID, C("CW", 512, 768)), (o, I50, x), (o, I50, C("WUV", 0, 256))])
            act(C("WR", 512, 768), o, AF.Identity, bias=MAGIC)

    def far_mm(c):
        return [(C("P6", c + 128 * s, c + 128 * s + 128), C("FX", 128 * s, 128 * s + 128), ID) for s in range(2)]

    def far(t):
        for s in range(2):
            tt(C("FX", 128 * s, 128 * s + 128), IND(C("CK5", 8 * s, 8 * s + 8), C("XL", 0, 8)), C("THX", 0, 128), ALU.is_ge)
        if t < NT - 1:
            group(far_mm(256))
            scan(A("PFAR"), C("P6", 256, 512), C("ZERO", 0, 256), ALU.add, ALU.add)

    def edits(t):
        last = t == NT - 1
        for k in range(2):
            group([(C("P%d" % (2 + k), 0, 320), A("OH", j), A("OL", j, slice(4 * k, 4 * k + 4))) for j in range(4)])
        act(C("FS", 0, 320), C("P2", 0, 320), AF.Copy)
        cp(C("FS", 320, 640), C("P3", 0, 320))
        for q in range(2):
            tt(C("BAD", 256 * q, 256 * q + 256), IND(A("FS"), C("LOL", 16 * q, 16 * q + 16)), C("THS", 256 * q, 256 * q + 256),
               ALU.is_gt)
        group(far_mm(0) + [(C("P6", 0, 256), NBO, C("BAD", 256 * q, 256 * q + 256)) for q in range(2)])
        group([(C("P1", 0, 16), sel(a, "SEL2"), C("BAD", 256 * q + a, 256 * q + 256, 16)) for q in range(2) for a in range(16)])
        ts(A("WANT"), C("P6", 0, 256), 1.0, ALU.is_equal)
        p_now, p_prev = C("P1C", 16, 272), C("P1C", 15, 271)
        scan(p_now, A("WANT"), A("C32"), ALU.add, ALU.min)
        if not last:
            group([(C("P0", 0, 256), ID, A("PFAR")), (C("P0", 0, 256), NID, p_now)])
            for j in range(5):
                act(C("JUNK", 256 * j, 256 * j + 256), C("P0", 0, 256), AF.Sign, bias=C("COL", 16 + j), scale=-1.0,
                    acc=C("RS", j))
            ts(C("RL", 0, 5), C("RS", 0, 5), 0.5, ALU.mult, 128.0, ALU.add)
            cp(A("SND%d" % t), IND(A("PKS%d" % t), C("RL", 0, 5)))
            op("G", ("send", t), [A("SND%d" % t)], [], 1500, 0, "none")
        for q in range(2):
            tt(C("OFT", 16 * q, 16 * q + 16), C("UVF", 16 * q, 16 * q + 16), C("P1", 0, 16), ALU.add)
        tt(C("OFT", 32, 64), C("OFT", 0, 32), A("DL"), ALU.min)
        cp(A("OFL"), C("OFT", 32, 64))
        for q in range(2):
            tt(C("MT", 256 * q, 256 * q + 256), IND(A("IDF"), C("UVL", 16 * q, 16 * q + 16)), C("TGS", 264 * q, 264 * q + 256),
               ALU.is_equal)
        group([(A("P5"), LA, A("EA")), (A("P5"), LT, A("MT"))])
        act(A("SG"), A("P5"), AF.Sign)
        group([(C("P6", 0, 256), ID, C("CN", 256 * t, 256 * t + 256)), (C("P6", 0, 256), I2K, p_now),
               (C("P6", 0, 256), NI2K, p_prev), (C("P6", 0, 256), ID, p_prev)])
        for q in range(2):
            tt(C("TP", 256 * q, 256 * q + 256), C("TGS", 264 * q, 264 * q + 256), C("P6", 0, 256), ALU.max)
        group([(A("P5"), NIB, A("SG")), (A("P5"), NID, A("TP"))])
        ts(IND(C("W", 0, 1792), A("OFL")), C("WR", 0, 512), 1.0, ALU.mult, -MAGIC, ALU.add)
        wsc = here()

        def lin(bank, const, age):
            items = [(A(bank), ID, const), (A(bank), ID, A("HALF")), (C(bank, 0, 256), NID, A("HH"))]
            items += [(C(bank, 256 * q, 256 * q + 256), NI32M, C("TT", 264 * q, 264 * q + 256)) for q in range(2)]
            if age:
                items.append((A(bank), ID, A("AG")))
            group(items + [(A(bank), IB, A("SG"))])
        if not last:
            lin("P3", A("C2"), True)
            act(A("Z2"), A("P5"), AF.Relu, bias=-30721.0)
            tt(A("M2"), A("Z2"), A("P3"), ALU.max)
            ts(IND(A("IDF"), A("OFL")), A("M2"), -1.0, ALU.mult, 2047.0, ALU.add)
            after(wsc)
        lin("P2", A("C1"), False)
        act(A("Z1"), A("P5"), AF.Relu, bias=-1.0)
        tt(A("M1"), A("Z1"), A("P2"), ALU.max)
        for j in range(2):
            act(C("JUNK", 1280 + 256 * j, 1536 + 256 * j), p_now, AF.Sign, bias=C("COL", 22 + j), scale=-1.0, acc=C("RS", 6 + j))
        sl = C("RL", 6, 8)
        ts(sl, C("RS", 6, 8), 0.5, ALU.mult, 128.0, ALU.add)
        c = L0 + NEW * t
        ts(C("W", c, c + NEW), IND(C("WR", 512, 776), sl), -MAGIC, ALU.add)
        ts(C("G1", 0, 32), IND(C("TT", 0, 264), sl), 1023.5, ALU.add, C("COL", 8), ALU.mult)
        ts(C("G1", 32, 64), IND(C("TGS", 0, 264), sl), C("DG", 1), ALU.mult, C("COL", 9), ALU.add)
        ts(C("G1", 64, 96), IND(C("TGS", 264, 528), sl), C("DG", 0), ALU.mult)
        tt(C("G1", 96, 128), C("G1", 0, 32), C("G1", 32, 64), ALU.add)
        tt(C("G1", 0, 32), C("G1", 96, 128), C("G1", 64, 96), ALU.add)
        if not last:
            ts(C("IDF", c, c + NEW), C("G1", 0, 32), 2047.0, ALU.min)
        cp(C("NB", c, c + NEW), C("G1", 0, 32))
        k = 1 if last else 4
        for j in range(k):
            ts(IND(A("NB"), C("OFL", 32 * j // k, 32 * (j + 1) // k)), C("M1", 512 * j // k, 512 * (j + 1) // k),
               -1.0, ALU.mult, 32767.0, ALU.add)
            prev["NB"].append(here())
        if last:
            after(wsc)

    def arrive(t):
        e = t - 1; c = 256 * t + 176
        op("R", ("arrive", e), [A("SND%d" % e)], [A("LND%d" % e)], 0, OPT["arrive"], "arr%d" % e)
        tt(A("NW"), IND(A("LND%d" % e), C("PERM", 0, 5)), C("PKO", 80 * e, 80 * e + 80), ALU.max)
        cp(C("NWI", 0, 80), A("NW"))
        ts(C("NWI", 160, 240), C("NWI", 0, 80), 255, ALU.bitwise_and)
        cp(C("X", c, c + 80), C("NWI", 160, 240))
        ts(C("NWI", 80, 160), C("NWI", 0, 80), 8, ALU.logical_shift_right, 2047, ALU.bitwise_and)
        cp(A("NWH"), C("NWI", 80, 160))
        group([(C("P6", 0, 5), sel(a), C("NWH", a, 80, 16)) for a in range(16)])
        ts(C("EL", 16 * t + 11, 16 * t + 16), C("P6", 0, 5), 1 / 1024, ALU.mult)
        ts(C("EF", 16 * t + 11, 16 * t + 16), C("P6", 0, 5), 1 / 1024, ALU.mult)
        XR = "XR%d" % (t % 2)
        act(C(XR, 2816, 3456), IND(C("X", c, c + 80), C("XL", 0, 40)), AF.Copy)
        cp(C(XR, 3456, 4096), IND(C("X", c, c + 80), C("XL", 40, 80)))
        if t < NT - 1:
            ts(C("PKS%d" % t, 176, 256), A("NW"), float(2 ** 19), ALU.add)

    for t in range(NT):
        for h in range(HOPS + 1):
            if h == HOPS:
                far(t); item(t, 0)
            near(t, h, 0)
            if h == 0 and t > 0:
                arrive(t)
            near(t, h, 1)
            if h == 0:
                if t == 0:
                    late_setup()
                if t + 1 < NT:
                    for i in range(16):
                        gcopy(C("XR%d" % ((t + 1) % 2), i, 2816, 16), C("X", 256 * t + 256, 256 * t + 432))
        item(t, 1)
        edits(t)
    act(A("WB"), C("W", 0, 1248), AF.Copy)
    dma("S", ("io", "yw", (ALL,)), A("WB"), 2500)
    dma("Y", ("io", "yn", (ALL,)), C("NB", 0, 1248), 3000)


def plan():
    ops = []
    build(ops)
    n = len(ops)
    SYNC = COST["sync"]
    wr, rd, bank = {}, {}, {}
    deps = []
    for i, o in enumerate(ops):
        d = {}
        for v in o["r"]:
            m = cols(v)[0]
            for j, mj in wr.get(v[1], []):
                if mj & m:
                    d[j] = True
        for v in o["w"]:
            m = cols(v)[0]
            for j, mj in wr.get(v[1], []) + rd.get(v[1], []):
                if mj & m and j != i:
                    d[j] = True
        for v in o["r"] + o["w"]:
            if psum(v):
                for j in bank.get(v[1], {}).values():
                    if j != i:
                        d.setdefault(j, False)
        for v in o["r"]:
            rd.setdefault(v[1], []).append((i, cols(v)[0]))
        for v in o["w"]:
            m = cols(v)[0]
            wr[v[1]] = [(j, mj) for j, mj in wr.get(v[1], []) if mj & ~m] + [(i, m)]
            rd[v[1]] = [(j, mj) for j, mj in rd.get(v[1], []) if mj & ~m or j == i]
        for v in o["r"] + o["w"]:
            if psum(v):
                bank.setdefault(v[1], {})[o["e"]] = i
        for j in o["after"]:
            d.setdefault(j, False)
        deps.append(d)

    def hard(i, j):
        if ops[j]["sem"] == "none":
            return False
        if ops[i]["e"] != ops[j]["e"] or ops[j]["sem"] or ops[i]["sem"]:
            return True
        return deps[i][j] and ops[i]["e"] != "P"
    succ = [[] for _ in range(n)]
    for i in range(n):
        for j in deps[i]:
            succ[j].append(i)
    prio = [0.0] * n
    for i in range(n - 1, -1, -1):
        p = 0.0
        for k in succ[i]:
            p = max(p, prio[k] + ((ops[i]["lat"] + SYNC) if hard(k, i) else 0.0))
        prio[i] = p + ops[i]["cost"]
    tail = ("S1", "NQ", "S2", "R8", "CT", "EX", "O16", "OFF")
    for i, o in enumerate(ops):
        nm = o["w"][0][1] if o["w"] else ""
        if nm[:-1] in tail or nm in ("CL", "UVL") or (o["e"] == "P" and o["r"][0][1][:2] in ("EX", "AB")):
            prio[i] += OPT["boost"]
        if nm == "OH" or (o["e"] == "P" and o["r"][0][1] == "SEL2"):
            prio[i] += OPT["hb"]
        if o["sem"] == "none":
            prio[i] += 1e9
    left = [len(d) for d in deps]
    est = [0.0] * n
    ready = {e: [] for e in "VSPGYR"}
    for i in range(n):
        if not left[i]:
            ready[ops[i]["e"]].append(i)
    free = {e: 0.0 for e in ready}
    order = {e: [] for e in ready}
    start = [0.0] * n
    seq = []
    for _ in range(n):
        best = None
        for e, r in ready.items():
            if not r:
                continue
            t0 = max(free[e], min(est[i] for i in r))
            c = max((i for i in r if est[i] <= t0 + OPT["look"]), key=lambda i: (prio[i], -i))
            if est[c] > t0:
                fill = [i for i in r if max(t0, est[i]) + ops[i]["cost"] <= est[c] + OPT["tol"] and est[i] < est[c]]
                if fill:
                    c = max(fill, key=lambda i: (prio[i], -i))
            t1 = max(free[e], est[c])
            if best is None or t1 < best[0]:
                best = (t1, e, c)
        t1, e, c = best
        ready[e].remove(c); order[e].append(c); seq.append(c); start[c] = t1
        free[e] = t1 + ops[c]["cost"]
        for k in succ[c]:
            est[k] = max(est[k], free[e] + ((ops[c]["lat"] + SYNC) if hard(k, c) else 0.0))
            left[k] -= 1
            if not left[k]:
                ready[ops[k]["e"]].append(k)
    count = {}
    tick = [None] * n
    for e in "VSPG":
        for i in order[e]:
            if not ops[i]["sem"]:
                count["s" + e] = count.get("s" + e, 0) + 1
                tick[i] = ("s" + e, count["s" + e])
    for i, o in enumerate(ops):
        if o["sem"] and o["sem"] != "none":
            tick[i] = (o["sem"], 16 if o["sem"][0] == "d" else -1)
            count[o["sem"]] = tick[i][1]
    known = {e: {} for e in ready}
    clock = [None] * n
    waits = [None] * n
    pos = {c: k for k, c in enumerate(seq)}
    for i in seq:
        e = ops[i]["e"]; kn = known[e]; w = {}
        for j in sorted(deps[i], key=lambda j: -pos[j]):
            if not hard(i, j):
                continue
            s, v = tick[j]
            if kn.get(s, 0) >= abs(v):
                continue
            w[s] = max(w.get(s, 0), abs(v)) if v > 0 else -1
            if ops[j]["e"] != "R":
                for s2, v2 in clock[j].items():
                    if kn.get(s2, 0) < v2:
                        kn[s2] = v2
            kn[s] = max(kn.get(s, 0), abs(v))
        waits[i] = w
        clock[i] = dict(kn)
    total = max(start[i] + ops[i]["cost"] + ops[i]["lat"] for i in range(n))
    return dict(ops=ops, seq=seq, tick=tick, waits=waits, count=count, total=total, start=start, deps=deps)


PLAN = []


def routes(T, topo):
    n = len(T.cores); out = []

    def share(eng, k):
        p = 1
        while 2 * p * k <= len(eng):
            p *= 2
        return [eng[i * p:(i + 1) * p] for i in range(k)]
    for q, src in enumerate(T.cores):
        dsts = [T.cores[(q + 1 + j) % n] for j in range(n - 1)]
        direct = [j for j, d in enumerate(dsts) if topo.may_write(src, d)]
        other = [j for j, d in enumerate(dsts) if j not in direct]
        off = topo.engines(src, dsts[direct[0]]) if direct else []
        mine = []
        for j, e in zip(direct, share(off, max(1, len(direct)))):
            mine.append((j, dsts[j], None, e[:4], None))
        if other:
            help_ = [c for c in topo.cores_of(src) if c != src and all(topo.may_write(c, dsts[j]) for j in other)]
            help_.sort(key=lambda c: topo.die(c) != topo.die(src))
            help_ = help_[:2]
            on = [e for e in topo.engines(src, help_[0]) if e not in off]
            per = {c: [j for k, j in enumerate(other) if help_[k % len(help_)] == c] for c in help_}
            for k, (j, e) in enumerate(zip(other, share(on, len(other)))):
                c = help_[k % len(help_)]
                e2 = share(topo.engines(c, dsts[j]), len(per[c]))[per[c].index(j)]
                mine.append((j, dsts[j], c, e, e2[:4]))
        out.append(mine)
    return out


def write(T, topo, src, dst, engines, sem, a, b):
    rid, pid = topo.addr(dst, src)
    return RemoteDMATransfer(dst_ids=[DstId(rid=rid, pnc=pid)], dma_engine_mask=sum(1 << e for e in engines),
                             remote_sem=T.sem[sem], src=a, dst=b)


def rank_program(g, core, T, topo):
    rank = T.rank_of(core)
    rt = routes(T, topo)
    if rank is None:
        mine = [r for q in rt for r in q if r[2] == core]
        if not mine:
            return
        sent = 0
        for e in range(NT - 1):
            g.wait_ge(T.sem["rel%d" % e], sum(len(r[3]) for r in mine))
            land = T["LND%d" % e]
            g.remote_dma_fused([write(T, topo, core, d, e2, "arr%d" % e, land[:, 16 * j:16 * j + 16], land[:, 16 * j:16 * j + 16])
                                for j, d, c, e1, e2 in mine], local_sem=T.sem.sent)
            sent += sum(len(r[4]) for r in mine)
        g.wait_ge(T.sem.sent, sent)
        return
    if not PLAN:
        PLAN.append(plan())
    P = PLAN[0]
    arrivals = sum(len(r[3] if r[2] is None else r[4]) for q in rt for r in q if r[1] == core)
    queue = {"V": g.vector, "S": g.scalar, "P": g.tensor, "G": g, "Y": g.sync}
    sent = 0
    for i in P["seq"]:
        o = P["ops"][i]
        if o["e"] == "R":
            continue
        for s, v in P["waits"][i].items():
            queue[o["e"]].wait_ge(T.sem[s], arrivals if v < 0 else v)
        if o["sem"] == "none":
            e = o["fn"][1]; snd, land = T["SND%d" % e], T["LND%d" % e]
            g.remote_dma_fused([write(T, topo, core, d if c is None else c, e1, ("arr%d" if c is None else "rel%d") % e,
                                      snd[:, 16 * j:16 * j + 16], land[:, 16 * j:16 * j + 16])
                                for j, d, c, e1, e2 in rt[rank]], local_sem=T.sem.sent)
            sent += sum(len(r[3]) for r in rt[rank])
            continue
        s, v = P["tick"][i]
        o["fn"](g, T).then_inc(T.sem[s], 16 if o["sem"] else 1)
    g.wait_ge(T.sem.sent, sent)
    for s, v in P["count"].items():
        if v > 0:
            g.wait_ge(T.sem[s], v)
